import numpy as np
import ml_dtypes


def mxq(x, axis, fmt="e4m3"):
    dtype, down = {"e4m3": (ml_dtypes.float8_e4m3fn, 7), "e5m2": (ml_dtypes.float8_e5m2, 14)}[fmt]
    v = np.moveaxis(np.asarray(x, np.float32).astype(ml_dtypes.bfloat16).astype(np.float64), axis, -1)
    blocks = v.reshape(v.shape[:-1] + (-1, 32))
    amax = np.abs(blocks).max(-1, keepdims=True)
    byte = np.maximum(np.where(amax > 0, np.frexp(amax)[1] - 1 + 127, 0) - down, 1)
    scale = np.exp2(byte - 127.0)
    codes = (blocks / scale).astype(np.float32).astype(dtype).astype(np.float64)
    return np.moveaxis((codes * scale).reshape(v.shape), -1, axis)


WIDE = False


def mx_kscale(k):
    if not WIDE:
        return np.ones(k)
    levels = np.array([24, -24, 12, -12, 0])
    if k % 512:
        return np.exp2(np.random.permutation(np.resize(levels, k // 32))).repeat(32)
    a = np.empty((k // 512, 16))
    for p in range(k // 512):
        a[p, :8] = np.random.permutation(np.resize(levels, 8))
        for g in range(8):
            far = levels[np.abs(levels - a[p, g]) >= 10]
            a[p, g + 8] = far[np.random.randint(len(far))]
    return np.exp2(a.ravel()).repeat(32)


def f64(x):
    return np.asarray(x).astype(np.float64)


def striped(idx):
    return np.tile(idx.reshape(-1, 16).T, (8, 1)).astype(np.uint16)


def unstriped(offs):
    return offs[:16].T.reshape(-1).astype(np.int64)


E2M1 = np.array([0.0, 0.5, 1.0, 1.5, 2.0, 3.0, 4.0, 6.0, -0.0, -0.5, -1.0, -1.5, -2.0, -3.0, -4.0, -6.0])


def pack_weight(w, fmt):
    k, n = w.shape
    w = f64(np.asarray(w, np.float32).astype(ml_dtypes.bfloat16)).reshape(k // 32, 32, n)
    amax = np.abs(w).max(1)
    if fmt == "e4m3":
        byte = np.frexp(amax)[1] - 1 + 127 - 7
    else:
        mant, ex = np.frexp(amax / 6.0)
        byte = np.where(mant > 0.5, ex, ex - 1) + 127
    byte = np.clip(np.where(amax > 0, byte, 1), 1, 254)
    scaled = (w * np.exp2(127.0 - byte)[:, None, :]).reshape(k, n).astype(np.float32)
    by_word = np.ascontiguousarray(scaled.reshape(k // 512, 128, 4, n).transpose(0, 1, 3, 2))
    if fmt == "e4m3":
        words = by_word.astype(ml_dtypes.float8_e4m3fn).view(np.uint8)
    else:
        c = by_word.astype(ml_dtypes.float4_e2m1fn).view(np.uint8) & 0xF
        words = (c[..., 0::2] | (c[..., 1::2] << 4)).reshape(k // 512, 128, 2 * n)
    return np.ascontiguousarray(words), np.ascontiguousarray(byte.astype(np.uint8).reshape(k // 512, 16, n))


def unpack_weight(words, scales, fmt):
    g, _, n = scales.shape
    words = np.ascontiguousarray(words).reshape(g, 128, n, -1)
    if fmt == "e4m3":
        vals = words.view(ml_dtypes.float8_e4m3fn).astype(np.float64)
    else:
        nib = np.empty((g, 128, n, 4), np.uint8)
        nib[..., 0::2] = words & 0xF
        nib[..., 1::2] = words >> 4
        vals = E2M1[nib]
    vals = vals * np.repeat(np.exp2(scales.astype(np.float64) - 127.0), 8, axis=1)[..., None]
    return vals.transpose(0, 1, 3, 2).reshape(g * 512, n)


K, F, N, T, J = 512, 1024, 128, 2048, 1024


def setup_inputs():
    n = np.random.standard_normal
    s = mx_kscale(K)[:, None]
    u = mx_kscale(F)[:, None]
    fb = np.abs(n((F, N))) / F / u
    p_tab = pack_weight(n((K, T)) * s, "e4m3")
    p_co = pack_weight(n((K, F)) / np.sqrt(K) / s, "e4m3")
    p_si = pack_weight(n((K, F)) / np.sqrt(K) / s, "e4m3")
    p_fb8 = pack_weight(fb[:512], "e4m3")
    p_fb4 = pack_weight(fb[512:], "e2m1")
    return {
        "tab_words": p_tab[0],
        "tab_scales": p_tab[1],
        "co_words": p_co[0],
        "co_scales": p_co[1],
        "si_words": p_si[0],
        "si_scales": p_si[1],
        "gn": (np.random.uniform(0.5, 2.0, F) * u[:, 0]).astype(np.float32),
        "fb8_words": p_fb8[0],
        "fb8_scales": p_fb8[1],
        "fb4_words": p_fb4[0],
        "fb4_scales": p_fb4[1],
        "offs": striped(np.random.permutation(T)[:J]),
    }


def reference(tab_words, tab_scales, co_words, co_scales, si_words, si_scales, gn, fb8_words, fb8_scales, fb4_words, fb4_scales, offs):
    idx = unstriped(offs)
    tab_ = unpack_weight(tab_words, tab_scales, "e4m3")[:, idx]
    co_ = unpack_weight(co_words, co_scales, "e4m3")
    si_ = unpack_weight(si_words, si_scales, "e4m3")
    re = co_.T @ tab_
    im = si_.T @ tab_
    h = f64(gn)[:, None] * np.sqrt((re) ** 2 + (im) ** 2)
    h_ = mxq(h, 0, "e4m3")
    fb8_ = unpack_weight(fb8_words, fb8_scales, "e4m3")
    fb4_ = unpack_weight(fb4_words, fb4_scales, "e2m1")
    y = fb8_.T @ h_[:512] + fb4_.T @ h_[512:]
    return y

@@ -1,0 +1,201 @@
+from contextlib import ExitStack
+
+import concourse.mybir as mybir
+from concourse.masks import make_identity
+
+K, F, N, T, J = 512, 1024, 128, 2048, 1024
+FLOPS = 2 * (2 * K * F * J + F * N * J)
+
+F32 = mybir.dt.float32
+BF16 = mybir.dt.bfloat16
+I32 = mybir.dt.int32
+U32 = mybir.dt.uint32
+U16 = mybir.dt.uint16
+U8 = mybir.dt.uint8
+FP8X4 = mybir.dt.float8_e4m3fn_x4
+FP4X4 = mybir.dt.float4_e2m1fn_x4
+ACT = mybir.ActivationFunctionType
+MULT = mybir.AluOpType.mult
+
+P = 128
+PACK = 4
+HALF = P * PACK
+HALVES = F // HALF
+TILES = J // P
+PIECE = 256
+CO_ROW, SI_ROW = 4, 8
+WIDE_TILES = 4
+
+
+def load_scale_rows(queues, plane, first_row, rows):
+    for q, queue in enumerate(queues):
+        queue.dma_start(
+            out=plane[32 * q + first_row : 32 * q + first_row + 4, :].bitcast(I32),
+            in_=rows[4 * q : 4 * q + 4, :].bitcast(I32),
+        )
+
+
+def tile_list_meltab_mix_mag_kernel(
+    tc, tab_words, tab_scales, co_words, co_scales, si_words, si_scales, gn,
+    fb8_words, fb8_scales, fb4_words, fb4_scales, offs, out,
+):
+    nc = tc.nc
+    with ExitStack() as ctx:
+        keep = ctx.enter_context(tc.tile_pool(name="keep", bufs=1))
+        ring = ctx.enter_context(tc.tile_pool(name="ring", bufs=3))
+        psum = ctx.enter_context(tc.psum_pool(name="psum", bufs=1))
+
+        offsets = keep.tile([P, J // 16], U16, name="offsets")
+        table = keep.tile([P, T], I32, name="table", align_bytes=64)
+        table_plane = keep.tile([P, T], U8, name="table_plane", align_bytes=64)
+        co_plane = keep.tile([P, F], U8, name="co_plane", align_bytes=64)
+        si_plane = keep.tile([P, F], U8, name="si_plane", align_bytes=64)
+        fb_planes = keep.tile([P, 2 * N], U8, name="fb_planes", align_bytes=64)
+        co = keep.tile([P, F], I32, name="co", align_bytes=64)
+        si = keep.tile([P, F], I32, name="si", align_bytes=64)
+        fb8 = keep.tile([P, N], I32, name="fb8", align_bytes=64)
+        fb4 = keep.tile([P, 2 * N], U8, name="fb4", align_bytes=64)
+        gain = keep.tile([P, HALVES, PACK], F32, name="gain")
+        identity = keep.tile([P, P], F32, name="identity")
+        warm_in = keep.tile([P, 1], F32, name="warm_in")
+        warm_out = keep.tile([P, 1], F32, name="warm_out")
+        h_codes = keep.tile([P, HALVES, J], U32, name="h_codes", align_bytes=64)
+        h_plane = keep.tile([P, HALVES, J], U8, name="h_plane", align_bytes=64)
+        result = keep.tile([P, J], F32, name="result")
+
+        fb8_plane = fb_planes[:, 0:N]
+        fb4_plane = fb_planes[:, N : 2 * N]
+
+        def words(dram):
+            return dram[0].rearrange("p n t -> p (n t)").bitcast(I32)
+
+        nc.vector.memset(table_plane[:].bitcast(I32), 0)
+        nc.vector.memset(warm_in[:], 1.0)
+        nc.gpsimd.memset(co_plane[:].bitcast(I32), 0)
+        nc.sync.dma_start(offsets[:], offs)
+        nc.sync.dma_start(out=gain[:], in_=gn.rearrange("(b m t) -> m b t", b=HALVES, t=PACK))
+        nc.sync.dma_start(out=table[:], in_=words(tab_words))
+        load_scale_rows([nc.scalar] * 4, table_plane, 0, tab_scales[0])
+        load_scale_rows([nc.scalar] * 3 + [nc.gpsimd], co_plane, CO_ROW, co_scales[0])
+        nc.scalar.activation(out=warm_out[:], in_=warm_in[:], func=ACT.Sqrt)
+        nc.gpsimd.dma_start(out=co[:], in_=words(co_words))
+        nc.gpsimd.memset(si_plane[:].bitcast(I32), 0)
+        nc.gpsimd.dma_start(out=si[:], in_=words(si_words))
+        load_scale_rows([nc.sync] * 4, si_plane, SI_ROW, si_scales[0])
+        make_identity(nc, identity[:])
+        nc.gpsimd.memset(fb_planes[:].bitcast(I32), 0)
+        nc.gpsimd.dma_start(out=fb8[:], in_=words(fb8_words))
+        nc.gpsimd.dma_start(out=fb4[:].bitcast(I32), in_=fb4_words[0].bitcast(I32))
+        load_scale_rows([nc.sync] * 4, fb8_plane, 0, fb8_scales[0])
+        load_scale_rows([nc.sync] * 4, fb4_plane, 0, fb4_scales[0])
+
+        picked = []
+
+        def gather(piece):
+            cols = offsets[:, piece * PIECE // 16 : (piece + 1) * PIECE // 16]
+            codes = keep.tile([P, PIECE], U32, name=f"picked_codes{piece}", align_bytes=64)
+            plane = keep.tile([P, PIECE], U8, name=f"picked_plane{piece}", align_bytes=64)
+            nc.vector.tensor_copy(plane[:], table_plane[:].indirect(cols))
+            nc.vector.tensor_copy(codes[:], table[:].bitcast(U32).indirect(cols))
+            picked.append((codes, plane))
+
+        def transform(k):
+            codes, plane = picked[k * P // PIECE]
+            tokens = slice(k * P % PIECE, k * P % PIECE + P)
+            parts = []
+            for weight, weight_plane, row in ((co, co_plane, CO_ROW), (si, si_plane, SI_ROW)):
+                for b in range(HALVES):
+                    freqs = slice(b * HALF, (b + 1) * HALF)
+                    part = psum.tile([P, HALF], F32, name="part", bufs=4)
+                    parts.append(part)
+                    nc.tensor.matmul_mx(
+                        out=part[:],
+                        lhsT=codes[:, tokens].bitcast(FP8X4),
+                        lhsT_scale=plane[:, tokens],
+                        rhs=weight[:, freqs].bitcast(FP8X4),
+                        rhs_scale=weight_plane[row:P, freqs],
+                        start=True,
+                        stop=True,
+                    )
+            return parts
+
+        def square(k, parts):
+            squares = ring.tile([P, 2 * HALVES, PACK, P], F32, name="squares", bufs=2)
+            for bank in range(2 * HALVES):
+                src = parts[bank][:].rearrange("p (m t) -> p t m", t=PACK)
+                if bank == 0 and k > 0:
+                    plain = ring.tile([P, PACK, P], F32, name="plain", bufs=2)
+                    nc.vector.tensor_copy(out=plain[:], in_=src)
+                    nc.vector.tensor_tensor(out=squares[:, bank], in0=src, in1=plain[:], op=MULT)
+                else:
+                    nc.scalar.activation(out=squares[:, bank], in_=src, func=ACT.Square)
+            return squares
+
+        def add_transposed(squares):
+            powers = []
+            for b in range(HALVES):
+                power = psum.tile([P, PACK, P], F32, name="power", bufs=3)
+                for t in range(PACK):
+                    for c in range(2):
+                        nc.tensor.matmul(
+                            out=power[:, t, :], lhsT=squares[:, HALVES * c + b, t, :], rhs=identity[:],
+                            start=(c == 0), stop=(c == 1), is_transpose=True,
+                        )
+                powers.append(power)
+            return powers
+
+        def magnitude(k, powers):
+            tokens = slice(k * P, (k + 1) * P)
+            hs = []
+            for b in range(HALVES):
+                mag = ring.tile([P, P, PACK], F32, name="mag")
+                nc.scalar.activation(out=mag[:], in_=powers[b][:].rearrange("p t j -> p j t"), func=ACT.Sqrt)
+                h = ring.tile([P, P, PACK], BF16, name="h", align_bytes=64)
+                nc.vector.tensor_tensor(
+                    out=h[:], in0=mag[:], in1=gain[:, b : b + 1, :].to_broadcast([P, P, PACK]), op=MULT
+                )
+                hs.append(h)
+            for b in range(HALVES):
+                nc.vector.quantize_mx(
+                    out=h_codes[:, b, tokens].bitcast(FP8X4),
+                    scales=h_plane[:, b, tokens],
+                    in_=hs[b][:].rearrange("p j t -> p (j t)"),
+                )
+
+        def filter_bank(tokens):
+            width = tokens.stop - tokens.start
+            y = psum.tile([P, width], F32, name="y")
+            nc.tensor.matmul_mx(
+                out=y[:], lhsT=fb8[:].bitcast(FP8X4), lhsT_scale=fb8_plane,
+                rhs=h_codes[:, 0, tokens].bitcast(FP8X4), rhs_scale=h_plane[:, 0, tokens],
+                start=True, stop=False,
+            )
+            nc.tensor.matmul_mx(
+                out=y[:], lhsT=fb4[:].bitcast(FP4X4), lhsT_scale=fb4_plane,
+                rhs=h_codes[:, 1, tokens].bitcast(FP8X4), rhs_scale=h_plane[:, 1, tokens],
+                start=False, stop=True,
+            )
+            nc.vector.tensor_copy(out=result[:, tokens], in_=y[:])
+            nc.sync.dma_start(out=out[:, tokens], in_=result[:, tokens])
+
+        def finish(k, powers):
+            magnitude(k, powers)
+            if k == WIDE_TILES - 1:
+                filter_bank(slice(0, WIDE_TILES * P))
+            elif k >= WIDE_TILES:
+                filter_bank(slice(k * P, (k + 1) * P))
+
+        gather(0)
+        parts = transform(0)
+        powers = None
+        for k in range(TILES):
+            squares = square(k, parts)
+            if k % 2 == 0 and k + 2 < TILES:
+                gather(k // 2 + 1)
+            if k + 1 < TILES:
+                parts = transform(k + 1)
+            previous = powers
+            powers = add_transposed(squares)
+            if k > 0:
+                finish(k - 1, previous)
+        finish(TILES - 1, powers)

@@ -24,11 +24,12 @@ HALVES = F // HALF
 TILES = J // P
 PIECE = 256
 CO_ROW, SI_ROW = 4, 8
-WIDE_TILES = 4
+PART_BANKS = 5
+STORES = ((0, 3), (4, 6), (7, 7))
 
 
-def load_scale_rows(queues, plane, first_row, rows):
-    for q, queue in enumerate(queues):
+def load_scale_rows(queue, plane, first_row, rows):
+    for q in range(4):
         queue.dma_start(
             out=plane[32 * q + first_row : 32 * q + first_row + 4, :].bitcast(I32),
             in_=rows[4 * q : 4 * q + 4, :].bitcast(I32),
@@ -59,8 +60,6 @@ def tile_list_meltab_mix_mag_kernel(
         identity = keep.tile([P, P], F32, name="identity")
         warm_in = keep.tile([P, 1], F32, name="warm_in")
         warm_out = keep.tile([P, 1], F32, name="warm_out")
-        h_codes = keep.tile([P, HALVES, J], U32, name="h_codes", align_bytes=64)
-        h_plane = keep.tile([P, HALVES, J], U8, name="h_plane", align_bytes=64)
         result = keep.tile([P, J], F32, name="result")
 
         fb8_plane = fb_planes[:, 0:N]
@@ -69,25 +68,27 @@ def tile_list_meltab_mix_mag_kernel(
         def words(dram):
             return dram[0].rearrange("p n t -> p (n t)").bitcast(I32)
 
+        si_words32 = words(si_words)
         nc.vector.memset(table_plane[:].bitcast(I32), 0)
         nc.vector.memset(warm_in[:], 1.0)
+        nc.vector.memset(si_plane[:].bitcast(I32), 0)
         nc.gpsimd.memset(co_plane[:].bitcast(I32), 0)
         nc.sync.dma_start(offsets[:], offs)
-        nc.sync.dma_start(out=gain[:], in_=gn.rearrange("(b m t) -> m b t", b=HALVES, t=PACK))
         nc.sync.dma_start(out=table[:], in_=words(tab_words))
-        load_scale_rows([nc.scalar] * 4, table_plane, 0, tab_scales[0])
-        load_scale_rows([nc.scalar] * 3 + [nc.gpsimd], co_plane, CO_ROW, co_scales[0])
+        load_scale_rows(nc.scalar, table_plane, 0, tab_scales[0])
+        load_scale_rows(nc.gpsimd, co_plane, CO_ROW, co_scales[0])
         nc.scalar.activation(out=warm_out[:], in_=warm_in[:], func=ACT.Sqrt)
-        nc.gpsimd.dma_start(out=co[:], in_=words(co_words))
-        nc.gpsimd.memset(si_plane[:].bitcast(I32), 0)
-        nc.gpsimd.dma_start(out=si[:], in_=words(si_words))
-        load_scale_rows([nc.sync] * 4, si_plane, SI_ROW, si_scales[0])
+        nc.sync.dma_start(out=co[:], in_=words(co_words))
+        nc.sync.dma_start(out=si[:, 0:HALF], in_=si_words32[:, 0:HALF])
+        load_scale_rows(nc.sync, si_plane, SI_ROW, si_scales[0])
+        nc.sync.dma_start(out=si[:, HALF:F], in_=si_words32[:, HALF:F])
         make_identity(nc, identity[:])
         nc.gpsimd.memset(fb_planes[:].bitcast(I32), 0)
-        nc.gpsimd.dma_start(out=fb8[:], in_=words(fb8_words))
-        nc.gpsimd.dma_start(out=fb4[:].bitcast(I32), in_=fb4_words[0].bitcast(I32))
-        load_scale_rows([nc.sync] * 4, fb8_plane, 0, fb8_scales[0])
-        load_scale_rows([nc.sync] * 4, fb4_plane, 0, fb4_scales[0])
+        nc.sync.dma_start(out=gain[:], in_=gn.rearrange("(b m t) -> m b t", b=HALVES, t=PACK))
+        nc.sync.dma_start(out=fb8[:], in_=words(fb8_words))
+        nc.sync.dma_start(out=fb4[:].bitcast(I32), in_=fb4_words[0].bitcast(I32))
+        load_scale_rows(nc.sync, fb8_plane, 0, fb8_scales[0])
+        load_scale_rows(nc.sync, fb4_plane, 0, fb4_scales[0])
 
         picked = []
 
@@ -106,7 +107,7 @@ def tile_list_meltab_mix_mag_kernel(
             for weight, weight_plane, row in ((co, co_plane, CO_ROW), (si, si_plane, SI_ROW)):
                 for b in range(HALVES):
                     freqs = slice(b * HALF, (b + 1) * HALF)
-                    part = psum.tile([P, HALF], F32, name="part", bufs=4)
+                    part = psum.tile([P, HALF], F32, name="part", bufs=PART_BANKS)
                     parts.append(part)
                     nc.tensor.matmul_mx(
                         out=part[:],
@@ -119,22 +120,20 @@ def tile_list_meltab_mix_mag_kernel(
                     )
             return parts
 
-        def square(k, parts):
-            squares = ring.tile([P, 2 * HALVES, PACK, P], F32, name="squares", bufs=2)
-            for bank in range(2 * HALVES):
-                src = parts[bank][:].rearrange("p (m t) -> p t m", t=PACK)
-                if bank == 0 and k > 0:
-                    plain = ring.tile([P, PACK, P], F32, name="plain", bufs=2)
-                    nc.vector.tensor_copy(out=plain[:], in_=src)
-                    nc.vector.tensor_tensor(out=squares[:, bank], in0=src, in1=plain[:], op=MULT)
-                else:
-                    nc.scalar.activation(out=squares[:, bank], in_=src, func=ACT.Square)
-            return squares
+        def by_slot(part):
+            return part[:].rearrange("p (m t) -> p t m", t=PACK)
 
-        def add_transposed(squares):
+        def square_on_scalar(k, parts, squares):
+            for bank in range(1 if k > 0 else 0, 2 * HALVES):
+                nc.scalar.activation(out=squares[:, bank], in_=by_slot(parts[bank]), func=ACT.Square)
+
+        def add_transposed(k, squares):
             powers = []
             for b in range(HALVES):
-                power = psum.tile([P, PACK, P], F32, name="power", bufs=3)
+                if k == TILES - 1:
+                    power = psum.tile([P, PACK, P], F32, name="part", bufs=PART_BANKS)
+                else:
+                    power = psum.tile([P, PACK, P], F32, name="power", bufs=2)
                 for t in range(PACK):
                     for c in range(2):
                         nc.tensor.matmul(
@@ -144,58 +143,87 @@ def tile_list_meltab_mix_mag_kernel(
                 powers.append(power)
             return powers
 
-        def magnitude(k, powers):
-            tokens = slice(k * P, (k + 1) * P)
-            hs = []
+        def magnitude(powers):
+            h = ring.tile([P, HALVES, P, PACK], BF16, name="h", align_bytes=64)
             for b in range(HALVES):
                 mag = ring.tile([P, P, PACK], F32, name="mag")
                 nc.scalar.activation(out=mag[:], in_=powers[b][:].rearrange("p t j -> p j t"), func=ACT.Sqrt)
-                h = ring.tile([P, P, PACK], BF16, name="h", align_bytes=64)
                 nc.vector.tensor_tensor(
-                    out=h[:], in0=mag[:], in1=gain[:, b : b + 1, :].to_broadcast([P, P, PACK]), op=MULT
+                    out=h[:, b], in0=mag[:], in1=gain[:, b : b + 1, :].to_broadcast([P, P, PACK]), op=MULT
                 )
-                hs.append(h)
-            for b in range(HALVES):
+            return h
+
+        def quantise(k, h):
+            codes = ring.tile([P, HALVES * P], U32, name="h_codes", align_bytes=64)
+            plane = ring.tile([P, HALVES * P], U8, name="h_plane", align_bytes=64)
+            flat = h[:].rearrange("p b j t -> p (b j t)")
+            pieces = HALVES if k == TILES - 1 else 1
+            width = HALVES * P // pieces
+            for i in range(pieces):
                 nc.vector.quantize_mx(
-                    out=h_codes[:, b, tokens].bitcast(FP8X4),
-                    scales=h_plane[:, b, tokens],
-                    in_=hs[b][:].rearrange("p j t -> p (j t)"),
+                    out=codes[:, i * width : (i + 1) * width].bitcast(FP8X4),
+                    scales=plane[:, i * width : (i + 1) * width],
+                    in_=flat[:, i * width * PACK : (i + 1) * width * PACK],
                 )
+            return codes, plane
 
-        def filter_bank(tokens):
-            width = tokens.stop - tokens.start
-            y = psum.tile([P, width], F32, name="y")
+        sums = {}
+
+        def filter_bank(k, codes, plane):
+            first, last = [(a, z) for a, z in STORES if a <= k <= z][0]
+            if k == first:
+                sums[first] = psum.tile([P, (last - first + 1) * P], F32, name="y")
+            cols = slice((k - first) * P, (k - first + 1) * P)
             nc.tensor.matmul_mx(
-                out=y[:], lhsT=fb8[:].bitcast(FP8X4), lhsT_scale=fb8_plane,
-                rhs=h_codes[:, 0, tokens].bitcast(FP8X4), rhs_scale=h_plane[:, 0, tokens],
-                start=True, stop=False,
+                out=sums[first][:, cols], lhsT=fb8[:].bitcast(FP8X4), lhsT_scale=fb8_plane,
+                rhs=codes[:, 0:P].bitcast(FP8X4), rhs_scale=plane[:, 0:P], start=True, stop=False,
             )
             nc.tensor.matmul_mx(
-                out=y[:], lhsT=fb4[:].bitcast(FP4X4), lhsT_scale=fb4_plane,
-                rhs=h_codes[:, 1, tokens].bitcast(FP8X4), rhs_scale=h_plane[:, 1, tokens],
-                start=False, stop=True,
+                out=sums[first][:, cols], lhsT=fb4[:].bitcast(FP4X4), lhsT_scale=fb4_plane,
+                rhs=codes[:, P : 2 * P].bitcast(FP8X4), rhs_scale=plane[:, P : 2 * P], start=False, stop=True,
             )
-            nc.vector.tensor_copy(out=result[:, tokens], in_=y[:])
-            nc.sync.dma_start(out=out[:, tokens], in_=result[:, tokens])
 
-        def finish(k, powers):
-            magnitude(k, powers)
-            if k == WIDE_TILES - 1:
-                filter_bank(slice(0, WIDE_TILES * P))
-            elif k >= WIDE_TILES:
-                filter_bank(slice(k * P, (k + 1) * P))
+        def store(k):
+            for first, last in STORES:
+                if k == last:
+                    tokens = slice(first * P, (last + 1) * P)
+                    if first == 0:
+                        nc.vector.tensor_copy(out=result[:, tokens], in_=sums[first][:])
+                    else:
+                        nc.scalar.copy(out=result[:, tokens], in_=sums[first][:])
+                    nc.sync.dma_start(out=out[:, tokens], in_=result[:, tokens])
 
         gather(0)
+        gather(1)
         parts = transform(0)
-        powers = None
+        squares = ring.tile([P, 2 * HALVES, PACK, P], F32, name="squares")
+        powers, hs, quantised = {}, {}, {}
         for k in range(TILES):
-            squares = square(k, parts)
-            if k % 2 == 0 and k + 2 < TILES:
-                gather(k // 2 + 1)
-            if k + 1 < TILES:
+            more = k + 1 < TILES
+            square_on_scalar(k, parts, squares)
+            if more:
                 parts = transform(k + 1)
-            previous = powers
-            powers = add_transposed(squares)
+                next_squares = ring.tile([P, 2 * HALVES, PACK, P], F32, name="squares")
+                plain = ring.tile([P, PACK, P], F32, name="plain")
+                nc.vector.tensor_copy(out=plain[:], in_=by_slot(parts[0]))
+            if k >= 2:
+                quantised[k - 2] = quantise(k - 2, hs[k - 2])
+            if more:
+                nc.vector.tensor_tensor(out=next_squares[:, 0], in0=by_slot(parts[0]), in1=plain[:], op=MULT)
+            if k < 2:
+                gather(k + 2)
+            if k >= 2 and more:
+                filter_bank(k - 2, *quantised[k - 2])
+            powers[k] = add_transposed(k, squares)
+            if not more:
+                filter_bank(k - 2, *quantised[k - 2])
             if k > 0:
-                finish(k - 1, previous)
-        finish(TILES - 1, powers)
+                hs[k - 1] = magnitude(powers[k - 1])
+            if k >= 2:
+                store(k - 2)
+            squares = next_squares
+        filter_bank(TILES - 2, *quantise(TILES - 2, hs[TILES - 2]))
+        last_h = magnitude(powers[TILES - 1])
+        store(TILES - 2)
+        filter_bank(TILES - 1, *quantise(TILES - 1, last_h))
+        store(TILES - 1)

@@ -28,8 +28,8 @@ PART_BANKS = 5
 STORES = ((0, 3), (4, 6), (7, 7))
 
 
-def load_scale_rows(queue, plane, first_row, rows):
-    for q in range(4):
+def load_scale_rows(queue, plane, first_row, rows, quadrants):
+    for q in quadrants:
         queue.dma_start(
             out=plane[32 * q + first_row : 32 * q + first_row + 4, :].bitcast(I32),
             in_=rows[4 * q : 4 * q + 4, :].bitcast(I32),
@@ -48,60 +48,71 @@ def tile_list_meltab_mix_mag_kernel(
 
         offsets = keep.tile([P, J // 16], U16, name="offsets")
         table = keep.tile([P, T], I32, name="table", align_bytes=64)
-        table_plane = keep.tile([P, T], U8, name="table_plane", align_bytes=64)
+        table_plane = keep.tile([P, T], U8, name="table_plane", tag="odd_codes", align_bytes=64)
         co_plane = keep.tile([P, F], U8, name="co_plane", align_bytes=64)
-        si_plane = keep.tile([P, F], U8, name="si_plane", align_bytes=64)
-        fb_planes = keep.tile([P, 2 * N], U8, name="fb_planes", align_bytes=64)
-        co = keep.tile([P, F], I32, name="co", align_bytes=64)
-        si = keep.tile([P, F], I32, name="si", align_bytes=64)
-        fb8 = keep.tile([P, N], I32, name="fb8", align_bytes=64)
-        fb4 = keep.tile([P, 2 * N], U8, name="fb4", align_bytes=64)
-        gain = keep.tile([P, HALVES, PACK], F32, name="gain")
         identity = keep.tile([P, P], F32, name="identity")
-        warm_in = keep.tile([P, 1], F32, name="warm_in")
-        warm_out = keep.tile([P, 1], F32, name="warm_out")
+        warm_in = keep.tile([P, 1], F32, name="warm_in", tag="weights", align_bytes=64)
+        warm_bias = keep.tile([P, 1], F32, name="warm_bias", tag="gain")
+        warm_out = keep.tile([P, 1], F32, name="warm_out", tag="si_plane", align_bytes=64)
         result = keep.tile([P, J], F32, name="result")
-
-        fb8_plane = fb_planes[:, 0:N]
-        fb4_plane = fb_planes[:, N : 2 * N]
 
         def words(dram):
             return dram[0].rearrange("p n t -> p (n t)").bitcast(I32)
 
-        si_words32 = words(si_words)
-        nc.vector.memset(table_plane[:].bitcast(I32), 0)
         nc.vector.memset(warm_in[:], 1.0)
-        nc.vector.memset(si_plane[:].bitcast(I32), 0)
-        nc.gpsimd.memset(co_plane[:].bitcast(I32), 0)
+        nc.vector.memset(warm_bias[:], 0.0)
+        nc.vector.memset(co_plane[:].bitcast(I32), 0)
+        nc.vector.memset(table_plane[:].bitcast(I32), 0)
+        nc.scalar.activation(out=warm_out[:], in_=warm_in[:], func=ACT.Sqrt, bias=warm_bias[:])
         nc.sync.dma_start(offsets[:], offs)
         nc.sync.dma_start(out=table[:], in_=words(tab_words))
-        load_scale_rows(nc.scalar, table_plane, 0, tab_scales[0])
-        load_scale_rows(nc.gpsimd, co_plane, CO_ROW, co_scales[0])
-        nc.scalar.activation(out=warm_out[:], in_=warm_in[:], func=ACT.Sqrt)
-        nc.sync.dma_start(out=co[:], in_=words(co_words))
-        nc.sync.dma_start(out=si[:, 0:HALF], in_=si_words32[:, 0:HALF])
-        load_scale_rows(nc.sync, si_plane, SI_ROW, si_scales[0])
-        nc.sync.dma_start(out=si[:, HALF:F], in_=si_words32[:, HALF:F])
+        load_scale_rows(nc.gpsimd, co_plane, CO_ROW, co_scales[0], range(0, 2))
+        load_scale_rows(nc.scalar, table_plane, 0, tab_scales[0], range(4))
+        load_scale_rows(nc.scalar, co_plane, CO_ROW, co_scales[0], range(2, 4))
         make_identity(nc, identity[:])
-        nc.gpsimd.memset(fb_planes[:].bitcast(I32), 0)
+
+        weights = keep.tile([P, 2, F], I32, name="weights", align_bytes=64)
+        si_plane = keep.tile([P, F], U8, name="si_plane", align_bytes=64)
+        gain = keep.tile([P, HALVES, PACK], F32, name="gain")
+        co, si = weights[:, 0, :], weights[:, 1, :]
+        nc.sync.dma_start(out=co, in_=words(co_words))
+        nc.sync.dma_start(out=si, in_=words(si_words))
         nc.sync.dma_start(out=gain[:], in_=gn.rearrange("(b m t) -> m b t", b=HALVES, t=PACK))
-        nc.sync.dma_start(out=fb8[:], in_=words(fb8_words))
-        nc.sync.dma_start(out=fb4[:].bitcast(I32), in_=fb4_words[0].bitcast(I32))
-        load_scale_rows(nc.sync, fb8_plane, 0, fb8_scales[0])
-        load_scale_rows(nc.sync, fb4_plane, 0, fb4_scales[0])
+        nc.vector.memset(si_plane[:].bitcast(I32), 0)
+        load_scale_rows(nc.scalar, si_plane, SI_ROW, si_scales[0], range(4))
 
-        picked = []
+        picked_codes, picked_planes = {}, {}
 
-        def gather(piece):
-            cols = offsets[:, piece * PIECE // 16 : (piece + 1) * PIECE // 16]
-            codes = keep.tile([P, PIECE], U32, name=f"picked_codes{piece}", align_bytes=64)
+        def piece_offsets(piece):
+            return offsets[:, piece * PIECE // 16 : (piece + 1) * PIECE // 16]
+
+        def gather_scales(piece):
             plane = keep.tile([P, PIECE], U8, name=f"picked_plane{piece}", align_bytes=64)
-            nc.vector.tensor_copy(plane[:], table_plane[:].indirect(cols))
-            nc.vector.tensor_copy(codes[:], table[:].bitcast(U32).indirect(cols))
-            picked.append((codes, plane))
+            nc.vector.tensor_copy(plane[:], table_plane[:].indirect(piece_offsets(piece)))
+            picked_planes[piece] = plane
+
+        def gather_words(piece):
+            tag = "odd_codes" if piece % 2 else "even_codes"
+            codes = keep.tile([P, PIECE], U32, name=f"picked_codes{piece}", tag=tag, align_bytes=64)
+            nc.vector.tensor_copy(codes[:], table[:].bitcast(U32).indirect(piece_offsets(piece)))
+            picked_codes[piece] = codes
+
+        filters = {}
+
+        def load_filters():
+            tile = keep.tile([P, 2 * N], I32, name="filters", tag="picked_plane0", align_bytes=64)
+            filters["fb8"] = tile[:, 0:N]
+            filters["fb4"] = tile[:, N : N + N // 2].bitcast(U8)
+            filters["fb8_plane"] = tile[:, N + N // 2 : N + N // 2 + N // 4].bitcast(U8)
+            filters["fb4_plane"] = tile[:, N + N // 2 + N // 4 : 2 * N].bitcast(U8)
+            nc.gpsimd.memset(tile[:], 0)
+            nc.sync.dma_start(out=filters["fb8"], in_=words(fb8_words))
+            nc.sync.dma_start(out=filters["fb4"].bitcast(I32), in_=fb4_words[0].bitcast(I32))
+            load_scale_rows(nc.sync, filters["fb8_plane"], 0, fb8_scales[0], range(4))
+            load_scale_rows(nc.sync, filters["fb4_plane"], 0, fb4_scales[0], range(4))
 
         def transform(k):
-            codes, plane = picked[k * P // PIECE]
+            codes, plane = picked_codes[k * P // PIECE], picked_planes[k * P // PIECE]
             tokens = slice(k * P % PIECE, k * P % PIECE + P)
             parts = []
             for weight, weight_plane, row in ((co, co_plane, CO_ROW), (si, si_plane, SI_ROW)):
@@ -175,11 +186,11 @@ def tile_list_meltab_mix_mag_kernel(
                 sums[first] = psum.tile([P, (last - first + 1) * P], F32, name="y")
             cols = slice((k - first) * P, (k - first + 1) * P)
             nc.tensor.matmul_mx(
-                out=sums[first][:, cols], lhsT=fb8[:].bitcast(FP8X4), lhsT_scale=fb8_plane,
+                out=sums[first][:, cols], lhsT=filters["fb8"].bitcast(FP8X4), lhsT_scale=filters["fb8_plane"],
                 rhs=codes[:, 0:P].bitcast(FP8X4), rhs_scale=plane[:, 0:P], start=True, stop=False,
             )
             nc.tensor.matmul_mx(
-                out=sums[first][:, cols], lhsT=fb4[:].bitcast(FP4X4), lhsT_scale=fb4_plane,
+                out=sums[first][:, cols], lhsT=filters["fb4"].bitcast(FP4X4), lhsT_scale=filters["fb4_plane"],
                 rhs=codes[:, P : 2 * P].bitcast(FP8X4), rhs_scale=plane[:, P : 2 * P], start=False, stop=True,
             )
 
@@ -193,9 +204,12 @@ def tile_list_meltab_mix_mag_kernel(
                         nc.scalar.copy(out=result[:, tokens], in_=sums[first][:])
                     nc.sync.dma_start(out=out[:, tokens], in_=result[:, tokens])
 
-        gather(0)
-        gather(1)
+        gather_scales(0)
+        gather_words(0)
         parts = transform(0)
+        for piece in range(1, J // PIECE):
+            gather_scales(piece)
+        gather_words(1)
         squares = ring.tile([P, 2 * HALVES, PACK, P], F32, name="squares")
         powers, hs, quantised = {}, {}, {}
         for k in range(TILES):
@@ -210,8 +224,10 @@ def tile_list_meltab_mix_mag_kernel(
                 quantised[k - 2] = quantise(k - 2, hs[k - 2])
             if more:
                 nc.vector.tensor_tensor(out=next_squares[:, 0], in0=by_slot(parts[0]), in1=plain[:], op=MULT)
-            if k < 2:
-                gather(k + 2)
+            if k == 0:
+                load_filters()
+            if k in (1, 3):
+                gather_words((k + 3) // 2)
             if k >= 2 and more:
                 filter_bank(k - 2, *quantised[k - 2])
             powers[k] = add_transposed(k, squares)

@@ -16,6 +16,7 @@ FP8X4 = mybir.dt.float8_e4m3fn_x4
 FP4X4 = mybir.dt.float4_e2m1fn_x4
 ACT = mybir.ActivationFunctionType
 MULT = mybir.AluOpType.mult
+ADD = mybir.AluOpType.add
 
 P = 128
 PACK = 4
@@ -25,6 +26,8 @@ TILES = J // P
 PIECE = 256
 CO_ROW, SI_ROW = 4, 8
 PART_BANKS = 5
+WARM_PASSES = 7
+GPSIMD_TILES = (2, 3, 4, 5)
 STORES = ((0, 3), (4, 6), (7, 7))
 
 
@@ -43,43 +46,48 @@ def tile_list_meltab_mix_mag_kernel(
     nc = tc.nc
     with ExitStack() as ctx:
         keep = ctx.enter_context(tc.tile_pool(name="keep", bufs=1))
-        ring = ctx.enter_context(tc.tile_pool(name="ring", bufs=3))
         psum = ctx.enter_context(tc.psum_pool(name="psum", bufs=1))
 
         offsets = keep.tile([P, J // 16], U16, name="offsets")
-        table = keep.tile([P, T], I32, name="table", align_bytes=64)
-        table_plane = keep.tile([P, T], U8, name="table_plane", tag="odd_codes", align_bytes=64)
+        co_zeros = keep.tile([P, F // 4], I32, name="co_zeros", tag="table", align_bytes=64)
+        si_zeros = keep.tile([P, F // 4], I32, name="si_zeros", tag="weights", align_bytes=64)
+        table_plane = keep.tile([P, T], U8, name="table_plane", align_bytes=64)
         co_plane = keep.tile([P, F], U8, name="co_plane", align_bytes=64)
+        si_plane = keep.tile([P, F], U8, name="si_plane", align_bytes=64)
+        co_first = keep.tile([P, HALF], I32, name="co_first", align_bytes=64)
         identity = keep.tile([P, P], F32, name="identity")
-        warm_in = keep.tile([P, 1], F32, name="warm_in", tag="weights", align_bytes=64)
-        warm_bias = keep.tile([P, 1], F32, name="warm_bias", tag="gain")
-        warm_out = keep.tile([P, 1], F32, name="warm_out", tag="si_plane", align_bytes=64)
+        warm_in = keep.tile([P, 1], F32, name="warm_in", tag="gain")
+        warm_out = keep.tile([P, 1], F32, name="warm_out")
         result = keep.tile([P, J], F32, name="result")
 
         def words(dram):
             return dram[0].rearrange("p n t -> p (n t)").bitcast(I32)
 
-        nc.vector.memset(warm_in[:], 1.0)
-        nc.vector.memset(warm_bias[:], 0.0)
-        nc.vector.memset(co_plane[:].bitcast(I32), 0)
+        nc.vector.memset(co_zeros[:], 0)
         nc.vector.memset(table_plane[:].bitcast(I32), 0)
-        nc.scalar.activation(out=warm_out[:], in_=warm_in[:], func=ACT.Sqrt, bias=warm_bias[:])
+        nc.vector.tensor_copy(out=co_plane[:].bitcast(I32), in_=co_zeros[:])
+        nc.vector.memset(si_zeros[:], 0)
+        nc.vector.memset(warm_in[:], 1.0)
+        nc.vector.tensor_copy(out=si_plane[:].bitcast(I32), in_=si_zeros[:])
         nc.sync.dma_start(offsets[:], offs)
+        nc.sync.dma_start(out=co_first[:], in_=words(co_words)[:, 0:HALF])
+        load_scale_rows(nc.scalar, table_plane, 0, tab_scales[0], range(0, 2))
+        load_scale_rows(nc.sync, table_plane, 0, tab_scales[0], range(2, 4))
+        table = keep.tile([P, T], I32, name="table", align_bytes=64)
         nc.sync.dma_start(out=table[:], in_=words(tab_words))
-        load_scale_rows(nc.gpsimd, co_plane, CO_ROW, co_scales[0], range(0, 2))
-        load_scale_rows(nc.scalar, table_plane, 0, tab_scales[0], range(4))
-        load_scale_rows(nc.scalar, co_plane, CO_ROW, co_scales[0], range(2, 4))
+        nc.scalar.activation(out=warm_out[:], in_=warm_in[:], func=ACT.Sqrt)
+        load_scale_rows(nc.scalar, co_plane, CO_ROW, co_scales[0], range(4))
+        load_scale_rows(nc.gpsimd, si_plane, SI_ROW, si_scales[0], range(0, 2))
+        load_scale_rows(nc.scalar, si_plane, SI_ROW, si_scales[0], range(2, 4))
         make_identity(nc, identity[:])
 
-        weights = keep.tile([P, 2, F], I32, name="weights", align_bytes=64)
-        si_plane = keep.tile([P, F], U8, name="si_plane", align_bytes=64)
+        later = keep.tile([P, 3 * HALF], I32, name="weights", align_bytes=64)
         gain = keep.tile([P, HALVES, PACK], F32, name="gain")
-        co, si = weights[:, 0, :], weights[:, 1, :]
-        nc.sync.dma_start(out=co, in_=words(co_words))
-        nc.sync.dma_start(out=si, in_=words(si_words))
-        nc.sync.dma_start(out=gain[:], in_=gn.rearrange("(b m t) -> m b t", b=HALVES, t=PACK))
-        nc.vector.memset(si_plane[:].bitcast(I32), 0)
-        load_scale_rows(nc.scalar, si_plane, SI_ROW, si_scales[0], range(4))
+        weights = {(0, 0): co_first[:], (1, 0): later[:, 0:HALF], (0, 1): later[:, HALF:F], (1, 1): later[:, F : 3 * HALF]}
+        nc.scalar.dma_start(out=weights[(1, 0)], in_=words(si_words)[:, 0:HALF])
+        nc.scalar.dma_start(out=weights[(0, 1)], in_=words(co_words)[:, HALF:F])
+        nc.scalar.dma_start(out=weights[(1, 1)], in_=words(si_words)[:, HALF:F])
+        nc.scalar.dma_start(out=gain[:], in_=gn.rearrange("(b m t) -> m b t", b=HALVES, t=PACK))
 
         picked_codes, picked_planes = {}, {}
 
@@ -92,8 +100,7 @@ def tile_list_meltab_mix_mag_kernel(
             picked_planes[piece] = plane
 
         def gather_words(piece):
-            tag = "odd_codes" if piece % 2 else "even_codes"
-            codes = keep.tile([P, PIECE], U32, name=f"picked_codes{piece}", tag=tag, align_bytes=64)
+            codes = keep.tile([P, PIECE], U32, name=f"picked_codes{piece}", align_bytes=64)
             nc.vector.tensor_copy(codes[:], table[:].bitcast(U32).indirect(piece_offsets(piece)))
             picked_codes[piece] = codes
 
@@ -111,78 +118,114 @@ def tile_list_meltab_mix_mag_kernel(
             load_scale_rows(nc.sync, filters["fb8_plane"], 0, fb8_scales[0], range(4))
             load_scale_rows(nc.sync, filters["fb4_plane"], 0, fb4_scales[0], range(4))
 
-        def transform(k):
+        parts, squares, plains, added, powers, mags, hs, quantised, sums = {}, {}, {}, {}, {}, {}, {}, {}, {}
+
+        def transform(k, halves=range(HALVES), kinds=range(2)):
             codes, plane = picked_codes[k * P // PIECE], picked_planes[k * P // PIECE]
             tokens = slice(k * P % PIECE, k * P % PIECE + P)
-            parts = []
-            for weight, weight_plane, row in ((co, co_plane, CO_ROW), (si, si_plane, SI_ROW)):
-                for b in range(HALVES):
-                    freqs = slice(b * HALF, (b + 1) * HALF)
-                    part = psum.tile([P, HALF], F32, name="part", bufs=PART_BANKS)
-                    parts.append(part)
-                    nc.tensor.matmul_mx(
-                        out=part[:],
-                        lhsT=codes[:, tokens].bitcast(FP8X4),
-                        lhsT_scale=plane[:, tokens],
-                        rhs=weight[:, freqs].bitcast(FP8X4),
-                        rhs_scale=weight_plane[row:P, freqs],
-                        start=True,
-                        stop=True,
+            for c, b in [(c, b) for b in halves for c in kinds]:
+                weight_plane, row = ((co_plane, CO_ROW), (si_plane, SI_ROW))[c]
+                freqs = slice(b * HALF, (b + 1) * HALF)
+                part = psum.tile([P, HALF], F32, name="part", bufs=PART_BANKS)
+                parts[(k, c, b)] = part[:].rearrange("p (m t) -> p t m", t=PACK)
+                nc.tensor.matmul_mx(
+                    out=part[:],
+                    lhsT=codes[:, tokens].bitcast(FP8X4),
+                    lhsT_scale=plane[:, tokens],
+                    rhs=weights[(c, b)].bitcast(FP8X4),
+                    rhs_scale=weight_plane[row:P, freqs],
+                    start=True,
+                    stop=True,
+                )
+
+        def warm_tensor():
+            scratch = psum.tile([P, PIECE], F32, name="power", bufs=2)
+            for i in range(WARM_PASSES):
+                nc.tensor.matmul_mx(
+                    out=scratch[:], lhsT=co_first[:, 0:P].bitcast(FP8X4), lhsT_scale=picked_planes[0][:, 0:P],
+                    rhs=co_first[:, 0:PIECE].bitcast(FP8X4), rhs_scale=picked_planes[1][:], start=True, stop=True,
+                )
+
+        def new_square(key):
+            squares[key] = keep.tile([P, PACK, P], F32, name="square%d_%d_%d" % key)
+            return squares[key]
+
+        def square_on_scalar(key):
+            nc.scalar.activation(out=new_square(key)[:], in_=parts[key], func=ACT.Square)
+
+        def copy_on_vector(key):
+            plains[key] = keep.tile([P, PACK, P], F32, name="plain%d_%d_%d" % key)
+            nc.vector.tensor_copy(out=plains[key][:], in_=parts[key])
+
+        def square_on_vector(key):
+            nc.vector.tensor_tensor(out=new_square(key)[:], in0=parts[key], in1=plains[key][:], op=MULT)
+
+        def add_on_gpsimd(k):
+            tag = f"h{k - 3}" if k >= 3 else f"mag{k - 2}_0"
+            added[k] = keep.tile([P, PACK, P], F32, name=f"added{k}", tag=tag, align_bytes=64)
+            for slots in (slice(0, PACK // 2), slice(PACK // 2, PACK)):
+                nc.gpsimd.tensor_tensor(
+                    out=added[k][:, slots], in0=squares[(k, 0, 0)][:, slots], in1=squares[(k, 1, 0)][:, slots], op=ADD
+                )
+
+        def add_transposed(k, b, terms, first=True, last=True):
+            if first and k == TILES - 1:
+                powers[(k, b)] = psum.tile([P, PACK, P], F32, name="part", bufs=PART_BANKS)
+            elif first:
+                powers[(k, b)] = psum.tile([P, PACK, P], F32, name="power", bufs=2)
+            for t in range(PACK):
+                for c, term in enumerate(terms):
+                    whole = first and last
+                    nc.tensor.matmul(
+                        out=powers[(k, b)][:, t, :], lhsT=term[:, t, :], rhs=identity[:],
+                        start=(c == 0 if whole else first and t == 0),
+                        stop=(c == len(terms) - 1 if whole else last and t == PACK - 1),
+                        is_transpose=True,
                     )
-            return parts
 
-        def by_slot(part):
-            return part[:].rearrange("p (m t) -> p t m", t=PACK)
+        def turn(k, b):
+            if b == 0 and k in added:
+                add_transposed(k, b, [added[k]])
+            else:
+                add_transposed(k, b, [squares[(k, c, b)] for c in (1, 0)])
 
-        def square_on_scalar(k, parts, squares):
-            for bank in range(1 if k > 0 else 0, 2 * HALVES):
-                nc.scalar.activation(out=squares[:, bank], in_=by_slot(parts[bank]), func=ACT.Square)
-
-        def add_transposed(k, squares):
-            powers = []
-            for b in range(HALVES):
-                if k == TILES - 1:
-                    power = psum.tile([P, PACK, P], F32, name="part", bufs=PART_BANKS)
-                else:
-                    power = psum.tile([P, PACK, P], F32, name="power", bufs=2)
-                for t in range(PACK):
-                    for c in range(2):
-                        nc.tensor.matmul(
-                            out=power[:, t, :], lhsT=squares[:, HALVES * c + b, t, :], rhs=identity[:],
-                            start=(c == 0), stop=(c == 1), is_transpose=True,
-                        )
-                powers.append(power)
-            return powers
-
-        def magnitude(powers):
-            h = ring.tile([P, HALVES, P, PACK], BF16, name="h", align_bytes=64)
-            for b in range(HALVES):
-                mag = ring.tile([P, P, PACK], F32, name="mag")
-                nc.scalar.activation(out=mag[:], in_=powers[b][:].rearrange("p t j -> p j t"), func=ACT.Sqrt)
-                nc.vector.tensor_tensor(
-                    out=h[:, b], in0=mag[:], in1=gain[:, b : b + 1, :].to_broadcast([P, P, PACK]), op=MULT
-                )
-            return h
-
-        def quantise(k, h):
-            codes = ring.tile([P, HALVES * P], U32, name="h_codes", align_bytes=64)
-            plane = ring.tile([P, HALVES * P], U8, name="h_plane", align_bytes=64)
-            flat = h[:].rearrange("p b j t -> p (b j t)")
-            pieces = HALVES if k == TILES - 1 else 1
-            width = HALVES * P // pieces
+        def root(k, b, pieces=1):
+            mags[(k, b)] = keep.tile([P, P, PACK], F32, name=f"mag{k}_{b}", align_bytes=64)
             for i in range(pieces):
-                nc.vector.quantize_mx(
-                    out=codes[:, i * width : (i + 1) * width].bitcast(FP8X4),
-                    scales=plane[:, i * width : (i + 1) * width],
-                    in_=flat[:, i * width * PACK : (i + 1) * width * PACK],
+                tokens = slice(i * P // pieces, (i + 1) * P // pieces)
+                nc.scalar.activation(
+                    out=mags[(k, b)][:, tokens], in_=powers[(k, b)][:].rearrange("p t j -> p j t")[:, tokens],
+                    func=ACT.Sqrt,
                 )
-            return codes, plane
 
-        sums = {}
+        def apply_gain(k, b, pieces=1):
+            if k not in hs:
+                hs[k] = keep.tile([P, HALVES, P, PACK], BF16, name=f"h{k}", align_bytes=64)
+                codes = keep.tile([P, HALVES * P], U32, name=f"h_codes{k}", align_bytes=64)
+                plane = keep.tile([P, HALVES * P], U8, name=f"h_plane{k}", align_bytes=64)
+                quantised[k] = (codes, plane)
+            for i in range(pieces):
+                tokens = slice(i * P // pieces, (i + 1) * P // pieces)
+                nc.vector.tensor_tensor(
+                    out=hs[k][:, b, tokens], in0=mags[(k, b)][:, tokens],
+                    in1=gain[:, b : b + 1, :].to_broadcast([P, P // pieces, PACK]), op=MULT,
+                )
 
-        def filter_bank(k, codes, plane):
+        def quantise(k, first_half=0, halves=HALVES):
+            codes, plane = quantised[k]
+            cols = slice(first_half * P, (first_half + halves) * P)
+            nc.vector.quantize_mx(
+                out=codes[:, cols].bitcast(FP8X4),
+                scales=plane[:, cols],
+                in_=hs[k][:, first_half : first_half + halves].rearrange("p b j t -> p (b j t)"),
+            )
+
+        def filter_bank(k):
+            codes, plane = quantised[k]
             first, last = [(a, z) for a, z in STORES if a <= k <= z][0]
-            if k == first:
+            if k == TILES - 1:
+                sums[first] = psum.tile([P, P], F32, name="power", bufs=2)
+            elif k == first:
                 sums[first] = psum.tile([P, (last - first + 1) * P], F32, name="y")
             cols = slice((k - first) * P, (k - first + 1) * P)
             nc.tensor.matmul_mx(
@@ -204,42 +247,92 @@ def tile_list_meltab_mix_mag_kernel(
                         nc.scalar.copy(out=result[:, tokens], in_=sums[first][:])
                     nc.sync.dma_start(out=out[:, tokens], in_=result[:, tokens])
 
-        gather_scales(0)
-        gather_words(0)
-        parts = transform(0)
-        for piece in range(1, J // PIECE):
+        last = TILES - 1
+        for piece in range(J // PIECE):
             gather_scales(piece)
-        gather_words(1)
-        squares = ring.tile([P, 2 * HALVES, PACK, P], F32, name="squares")
-        powers, hs, quantised = {}, {}, {}
-        for k in range(TILES):
-            more = k + 1 < TILES
-            square_on_scalar(k, parts, squares)
-            if more:
-                parts = transform(k + 1)
-                next_squares = ring.tile([P, 2 * HALVES, PACK, P], F32, name="squares")
-                plain = ring.tile([P, PACK, P], F32, name="plain")
-                nc.vector.tensor_copy(out=plain[:], in_=by_slot(parts[0]))
-            if k >= 2:
-                quantised[k - 2] = quantise(k - 2, hs[k - 2])
-            if more:
-                nc.vector.tensor_tensor(out=next_squares[:, 0], in0=by_slot(parts[0]), in1=plain[:], op=MULT)
-            if k == 0:
-                load_filters()
-            if k in (1, 3):
-                gather_words((k + 3) // 2)
-            if k >= 2 and more:
-                filter_bank(k - 2, *quantised[k - 2])
-            powers[k] = add_transposed(k, squares)
-            if not more:
-                filter_bank(k - 2, *quantised[k - 2])
-            if k > 0:
-                hs[k - 1] = magnitude(powers[k - 1])
-            if k >= 2:
-                store(k - 2)
-            squares = next_squares
-        filter_bank(TILES - 2, *quantise(TILES - 2, hs[TILES - 2]))
-        last_h = magnitude(powers[TILES - 1])
-        store(TILES - 2)
-        filter_bank(TILES - 1, *quantise(TILES - 1, last_h))
-        store(TILES - 1)
+        warm_tensor()
+        gather_words(0)
+        transform(0, [0])
+        transform(1, [0])
+        for piece in range(1, J // PIECE):
+            gather_words(piece)
+        square_on_scalar((0, 0, 0))
+        square_on_scalar((0, 1, 0))
+        copy_on_vector((1, 0, 0))
+        transform(0, [1])
+        square_on_scalar((1, 1, 0))
+        square_on_vector((1, 0, 0))
+        transform(1, [1], [0])
+        turn(0, 0)
+        copy_on_vector((0, 0, 1))
+        square_on_scalar((0, 1, 1))
+        square_on_vector((0, 0, 1))
+        transform(1, [1], [1])
+        root(0, 0)
+        turn(1, 0)
+        copy_on_vector((1, 0, 1))
+        square_on_scalar((1, 1, 1))
+        apply_gain(0, 0)
+        square_on_vector((1, 0, 1))
+        transform(2)
+        load_filters()
+        root(1, 0)
+        turn(0, 1)
+        root(0, 1)
+        for k in range(2, last):
+            copy_on_vector((k, 0, 0))
+            square_on_scalar((k, 1, 0))
+            turn(k - 1, 1)
+            apply_gain(k - 2, 1)
+            if k >= 4:
+                root(k - 2, 0)
+            square_on_vector((k, 0, 0))
+            square_on_scalar((k, 0, 1))
+            if k >= 3:
+                quantise(k - 3)
+            if k in GPSIMD_TILES:
+                add_on_gpsimd(k)
+            square_on_scalar((k, 1, 1))
+            if k >= 3:
+                apply_gain(k - 2, 0)
+            transform(k + 1, [0])
+            transform(k + 1, [1], [0])
+            if k >= 3:
+                turn(k - 1, 0)
+            transform(k + 1, [1], [1])
+            if k >= 4:
+                filter_bank(k - 4)
+            root(k - 1, 1)
+        square_on_scalar((last, 0, 0))
+        turn(last - 1, 1)
+        apply_gain(last - 2, 1)
+        root(last - 2, 0)
+        quantise(last - 3)
+        turn(last - 1, 0)
+        square_on_scalar((last, 1, 0))
+        apply_gain(last - 2, 0)
+        filter_bank(last - 4)
+        store(last - 4)
+        root(last - 1, 1)
+        quantise(last - 2)
+        square_on_scalar((last, 0, 1))
+        turn(last, 0)
+        root(last - 1, 0)
+        add_transposed(last, 1, [squares[(last, 0, 1)]], last=False)
+        apply_gain(last - 1, 1)
+        square_on_scalar((last, 1, 1))
+        add_transposed(last, 1, [squares[(last, 1, 1)]], first=False)
+        filter_bank(last - 3)
+        filter_bank(last - 2)
+        apply_gain(last - 1, 0)
+        root(last, 0)
+        quantise(last - 1)
+        root(last, 1, 2)
+        apply_gain(last, 0)
+        filter_bank(last - 1)
+        quantise(last, 0, 1)
+        apply_gain(last, 1, 2)
+        store(last - 1)
+        quantise(last, 1, 1)
+        filter_bank(last)
+        store(last)

@@ -26,8 +26,9 @@ TILES = J // P
 PIECE = 256
 CO_ROW, SI_ROW = 4, 8
 PART_BANKS = 5
+EDGE = 16
 WARM_PASSES = 7
-GPSIMD_TILES = (2, 3, 4, 5)
+GPSIMD_TILES = ()
 STORES = ((0, 3), (4, 6), (7, 7))
 
 
@@ -49,8 +50,8 @@ def tile_list_meltab_mix_mag_kernel(
         psum = ctx.enter_context(tc.psum_pool(name="psum", bufs=1))
 
         offsets = keep.tile([P, J // 16], U16, name="offsets")
-        co_zeros = keep.tile([P, F // 4], I32, name="co_zeros", tag="table", align_bytes=64)
-        si_zeros = keep.tile([P, F // 4], I32, name="si_zeros", tag="weights", align_bytes=64)
+        left_zeros = keep.tile([P, EDGE], I32, name="left_zeros", tag="table", align_bytes=64)
+        right_zeros = keep.tile([P, EDGE], I32, name="right_zeros", tag="later", align_bytes=64)
         table_plane = keep.tile([P, T], U8, name="table_plane", align_bytes=64)
         co_plane = keep.tile([P, F], U8, name="co_plane", align_bytes=64)
         si_plane = keep.tile([P, F], U8, name="si_plane", align_bytes=64)
@@ -63,31 +64,36 @@ def tile_list_meltab_mix_mag_kernel(
         def words(dram):
             return dram[0].rearrange("p n t -> p (n t)").bitcast(I32)
 
-        nc.vector.memset(co_zeros[:], 0)
+        nc.vector.memset(co_plane[0:96, :].bitcast(I32), 0)
+        nc.vector.memset(left_zeros[:], 0)
+        nc.vector.memset(right_zeros[:], 0)
         nc.vector.memset(table_plane[:].bitcast(I32), 0)
-        nc.vector.tensor_copy(out=co_plane[:].bitcast(I32), in_=co_zeros[:])
-        nc.vector.memset(si_zeros[:], 0)
+        si_plane32 = si_plane[:].bitcast(I32)
+        nc.vector.tensor_copy(out=si_plane32[:, 0:EDGE], in_=left_zeros[:])
+        nc.vector.tensor_copy(out=si_plane32[:, EDGE : 2 * EDGE], in_=right_zeros[:])
+        nc.vector.memset(si_plane32[:, 2 * EDGE : F // 4], 0)
+        nc.vector.memset(co_plane[96:P, :].bitcast(I32), 0)
         nc.vector.memset(warm_in[:], 1.0)
-        nc.vector.tensor_copy(out=si_plane[:].bitcast(I32), in_=si_zeros[:])
         nc.sync.dma_start(offsets[:], offs)
         nc.sync.dma_start(out=co_first[:], in_=words(co_words)[:, 0:HALF])
+        load_scale_rows(nc.gpsimd, co_plane, CO_ROW, co_scales[0], range(0, 2))
+        load_scale_rows(nc.scalar, co_plane, CO_ROW, co_scales[0], range(2, 3))
         load_scale_rows(nc.scalar, table_plane, 0, tab_scales[0], range(0, 2))
         load_scale_rows(nc.sync, table_plane, 0, tab_scales[0], range(2, 4))
         table = keep.tile([P, T], I32, name="table", align_bytes=64)
         nc.sync.dma_start(out=table[:], in_=words(tab_words))
         nc.scalar.activation(out=warm_out[:], in_=warm_in[:], func=ACT.Sqrt)
-        load_scale_rows(nc.scalar, co_plane, CO_ROW, co_scales[0], range(4))
-        load_scale_rows(nc.gpsimd, si_plane, SI_ROW, si_scales[0], range(0, 2))
-        load_scale_rows(nc.scalar, si_plane, SI_ROW, si_scales[0], range(2, 4))
+        load_scale_rows(nc.scalar, co_plane, CO_ROW, co_scales[0], range(3, 4))
+        load_scale_rows(nc.sync, si_plane, SI_ROW, si_scales[0], range(4))
         make_identity(nc, identity[:])
 
-        later = keep.tile([P, 3 * HALF], I32, name="weights", align_bytes=64)
+        later = keep.tile([P, 3 * HALF], I32, name="later", align_bytes=64)
         gain = keep.tile([P, HALVES, PACK], F32, name="gain")
         weights = {(0, 0): co_first[:], (1, 0): later[:, 0:HALF], (0, 1): later[:, HALF:F], (1, 1): later[:, F : 3 * HALF]}
-        nc.scalar.dma_start(out=weights[(1, 0)], in_=words(si_words)[:, 0:HALF])
-        nc.scalar.dma_start(out=weights[(0, 1)], in_=words(co_words)[:, HALF:F])
-        nc.scalar.dma_start(out=weights[(1, 1)], in_=words(si_words)[:, HALF:F])
-        nc.scalar.dma_start(out=gain[:], in_=gn.rearrange("(b m t) -> m b t", b=HALVES, t=PACK))
+        nc.sync.dma_start(out=weights[(1, 0)], in_=words(si_words)[:, 0:HALF])
+        nc.sync.dma_start(out=weights[(0, 1)], in_=words(co_words)[:, HALF:F])
+        nc.sync.dma_start(out=weights[(1, 1)], in_=words(si_words)[:, HALF:F])
+        nc.sync.dma_start(out=gain[:], in_=gn.rearrange("(b m t) -> m b t", b=HALVES, t=PACK))
 
         picked_codes, picked_planes = {}, {}
 
@@ -283,32 +289,27 @@ def tile_list_meltab_mix_mag_kernel(
             copy_on_vector((k, 0, 0))
             square_on_scalar((k, 1, 0))
             turn(k - 1, 1)
+            if k >= 3:
+                turn(k - 1, 0)
             apply_gain(k - 2, 1)
-            if k >= 4:
-                root(k - 2, 0)
             square_on_vector((k, 0, 0))
             square_on_scalar((k, 0, 1))
             if k >= 3:
                 quantise(k - 3)
-            if k in GPSIMD_TILES:
-                add_on_gpsimd(k)
             square_on_scalar((k, 1, 1))
             if k >= 3:
                 apply_gain(k - 2, 0)
-            transform(k + 1, [0])
-            transform(k + 1, [1], [0])
-            if k >= 3:
-                turn(k - 1, 0)
-            transform(k + 1, [1], [1])
             if k >= 4:
                 filter_bank(k - 4)
+            transform(k + 1)
             root(k - 1, 1)
+            if k >= 3:
+                root(k - 1, 0)
         square_on_scalar((last, 0, 0))
         turn(last - 1, 1)
-        apply_gain(last - 2, 1)
-        root(last - 2, 0)
-        quantise(last - 3)
         turn(last - 1, 0)
+        apply_gain(last - 2, 1)
+        quantise(last - 3)
         square_on_scalar((last, 1, 0))
         apply_gain(last - 2, 0)
         filter_bank(last - 4)

@@ -1,7 +1,6 @@
 from contextlib import ExitStack
 
 import concourse.mybir as mybir
-from concourse.masks import make_identity
 
 K, F, N, T, J = 512, 1024, 128, 2048, 1024
 FLOPS = 2 * (2 * K * F * J + F * N * J)
@@ -25,8 +24,9 @@ HALVES = F // HALF
 TILES = J // P
 PIECE = 256
 CO_ROW, SI_ROW = 4, 8
-PART_BANKS = 5
+PART_BANKS = 6
 EDGE = 16
+WIDE = 4
 WARM_PASSES = 7
 GPSIMD_TILES = ()
 STORES = ((0, 3), (4, 6), (7, 7))
@@ -74,6 +74,7 @@ def tile_list_meltab_mix_mag_kernel(
         nc.vector.memset(si_plane32[:, 2 * EDGE : F // 4], 0)
         nc.vector.memset(co_plane[96:P, :].bitcast(I32), 0)
         nc.vector.memset(warm_in[:], 1.0)
+        nc.vector.memset(identity[:], 0.0)
         nc.sync.dma_start(offsets[:], offs)
         nc.sync.dma_start(out=co_first[:], in_=words(co_words)[:, 0:HALF])
         load_scale_rows(nc.gpsimd, co_plane, CO_ROW, co_scales[0], range(0, 2))
@@ -85,7 +86,10 @@ def tile_list_meltab_mix_mag_kernel(
         nc.scalar.activation(out=warm_out[:], in_=warm_in[:], func=ACT.Sqrt)
         load_scale_rows(nc.scalar, co_plane, CO_ROW, co_scales[0], range(3, 4))
         load_scale_rows(nc.sync, si_plane, SI_ROW, si_scales[0], range(4))
-        make_identity(nc, identity[:])
+        nc.gpsimd.affine_select(
+            out=identity[:], in_=identity[:], pattern=[[-1, P]], compare_op=mybir.AluOpType.not_equal, fill=1.0,
+            base=0, channel_multiplier=1,
+        )
 
         later = keep.tile([P, 3 * HALF], I32, name="later", align_bytes=64)
         gain = keep.tile([P, HALVES, PACK], F32, name="gain")
@@ -204,18 +208,31 @@ def tile_list_meltab_mix_mag_kernel(
                     func=ACT.Sqrt,
                 )
 
+        wide_h = [keep.tile([P, WIDE, P, PACK], BF16, name=f"wide_h{b}", align_bytes=64) for b in range(HALVES)]
+        wide_codes = [keep.tile([P, WIDE * P], U32, name=f"wide_codes{b}", align_bytes=64) for b in range(HALVES)]
+        wide_plane = [keep.tile([P, WIDE * P], U8, name=f"wide_plane{b}", align_bytes=64) for b in range(HALVES)]
+
         def apply_gain(k, b, pieces=1):
-            if k not in hs:
+            if k >= WIDE and k not in hs:
                 hs[k] = keep.tile([P, HALVES, P, PACK], BF16, name=f"h{k}", align_bytes=64)
                 codes = keep.tile([P, HALVES * P], U32, name=f"h_codes{k}", align_bytes=64)
                 plane = keep.tile([P, HALVES * P], U8, name=f"h_plane{k}", align_bytes=64)
                 quantised[k] = (codes, plane)
+            h = wide_h[b][:, k] if k < WIDE else hs[k][:, b]
             for i in range(pieces):
                 tokens = slice(i * P // pieces, (i + 1) * P // pieces)
                 nc.vector.tensor_tensor(
-                    out=hs[k][:, b, tokens], in0=mags[(k, b)][:, tokens],
+                    out=h[:, tokens], in0=mags[(k, b)][:, tokens],
                     in1=gain[:, b : b + 1, :].to_broadcast([P, P // pieces, PACK]), op=MULT,
                 )
+
+        def quantise_pair(k, b):
+            cols = slice(k * P, (k + 2) * P)
+            nc.vector.quantize_mx(
+                out=wide_codes[b][:, cols].bitcast(FP8X4),
+                scales=wide_plane[b][:, cols],
+                in_=wide_h[b][:, k : k + 2].rearrange("p k j t -> p (k j t)"),
+            )
 
         def quantise(k, first_half=0, halves=HALVES):
             codes, plane = quantised[k]
@@ -226,22 +243,29 @@ def tile_list_meltab_mix_mag_kernel(
                 in_=hs[k][:, first_half : first_half + halves].rearrange("p b j t -> p (b j t)"),
             )
 
+        def filter_passes(y, low, low_plane, high, high_plane):
+            nc.tensor.matmul_mx(
+                out=y, lhsT=filters["fb8"].bitcast(FP8X4), lhsT_scale=filters["fb8_plane"],
+                rhs=low.bitcast(FP8X4), rhs_scale=low_plane, start=True, stop=False,
+            )
+            nc.tensor.matmul_mx(
+                out=y, lhsT=filters["fb4"].bitcast(FP4X4), lhsT_scale=filters["fb4_plane"],
+                rhs=high.bitcast(FP8X4), rhs_scale=high_plane, start=False, stop=True,
+            )
+
+        def filter_wide():
+            sums[0] = psum.tile([P, WIDE * P], F32, name="part", bufs=PART_BANKS)
+            filter_passes(sums[0][:], wide_codes[0][:], wide_plane[0][:], wide_codes[1][:], wide_plane[1][:])
+
         def filter_bank(k):
             codes, plane = quantised[k]
             first, last = [(a, z) for a, z in STORES if a <= k <= z][0]
             if k == TILES - 1:
                 sums[first] = psum.tile([P, P], F32, name="power", bufs=2)
             elif k == first:
-                sums[first] = psum.tile([P, (last - first + 1) * P], F32, name="y")
+                sums[first] = psum.tile([P, (last - first + 1) * P], F32, name="part", bufs=PART_BANKS)
             cols = slice((k - first) * P, (k - first + 1) * P)
-            nc.tensor.matmul_mx(
-                out=sums[first][:, cols], lhsT=filters["fb8"].bitcast(FP8X4), lhsT_scale=filters["fb8_plane"],
-                rhs=codes[:, 0:P].bitcast(FP8X4), rhs_scale=plane[:, 0:P], start=True, stop=False,
-            )
-            nc.tensor.matmul_mx(
-                out=sums[first][:, cols], lhsT=filters["fb4"].bitcast(FP4X4), lhsT_scale=filters["fb4_plane"],
-                rhs=codes[:, P : 2 * P].bitcast(FP8X4), rhs_scale=plane[:, P : 2 * P], start=False, stop=True,
-            )
+            filter_passes(sums[first][:, cols], codes[:, 0:P], plane[:, 0:P], codes[:, P : 2 * P], plane[:, P : 2 * P])
 
         def store(k):
             for first, last in STORES:
@@ -257,83 +281,93 @@ def tile_list_meltab_mix_mag_kernel(
         for piece in range(J // PIECE):
             gather_scales(piece)
         warm_tensor()
-        gather_words(0)
+        for piece in range(J // PIECE):
+            gather_words(piece)
         transform(0, [0])
         transform(1, [0])
-        for piece in range(1, J // PIECE):
-            gather_words(piece)
+        transform(2, [0], [0])
         square_on_scalar((0, 0, 0))
+        transform(2, [0], [1])
         square_on_scalar((0, 1, 0))
         copy_on_vector((1, 0, 0))
-        transform(0, [1])
+        transform(0, [1], [0])
+        copy_on_vector((2, 0, 0))
         square_on_scalar((1, 1, 0))
         square_on_vector((1, 0, 0))
-        transform(1, [1], [0])
         turn(0, 0)
-        copy_on_vector((0, 0, 1))
-        square_on_scalar((0, 1, 1))
-        square_on_vector((0, 0, 1))
+        transform(1, [1], [0])
+        square_on_vector((2, 0, 0))
+        square_on_scalar((2, 1, 0))
+        transform(0, [1], [1])
         transform(1, [1], [1])
+        copy_on_vector((0, 0, 1))
         root(0, 0)
         turn(1, 0)
         copy_on_vector((1, 0, 1))
+        square_on_scalar((0, 1, 1))
+        square_on_vector((0, 0, 1))
+        transform(2, [1])
+        root(1, 0)
+        square_on_vector((1, 0, 1))
+        turn(2, 0)
         square_on_scalar((1, 1, 1))
         apply_gain(0, 0)
-        square_on_vector((1, 0, 1))
-        transform(2)
-        load_filters()
-        root(1, 0)
+        square_on_scalar((2, 0, 1))
         turn(0, 1)
+        root(2, 0)
+        apply_gain(1, 0)
+        square_on_scalar((2, 1, 1))
+        transform(3)
+        load_filters()
         root(0, 1)
-        for k in range(2, last):
+        early_sums = {3: ((1, 1), (2, 1))}
+        early_gains = {3: ((0, 1), (2, 0)), 4: ((1, 1), (2, 1))}
+        for k in range(3, last):
+            sums_now = early_sums.get(k, ((k - 1, 1), (k - 1, 0)))
+            gains_now = early_gains.get(k, ((k - 2, 1), (k - 2, 0)))
             copy_on_vector((k, 0, 0))
             square_on_scalar((k, 1, 0))
-            turn(k - 1, 1)
-            if k >= 3:
-                turn(k - 1, 0)
-            apply_gain(k - 2, 1)
+            turn(*sums_now[0])
+            turn(*sums_now[1])
+            apply_gain(*gains_now[0])
             square_on_vector((k, 0, 0))
             square_on_scalar((k, 0, 1))
-            if k >= 3:
-                quantise(k - 3)
+            quantise_pair(*{3: (0, 0), 4: (0, 1), 5: (2, 1), 6: (2, 0)}[k])
             square_on_scalar((k, 1, 1))
-            if k >= 3:
-                apply_gain(k - 2, 0)
-            if k >= 4:
-                filter_bank(k - 4)
-            transform(k + 1)
-            root(k - 1, 1)
-            if k >= 3:
-                root(k - 1, 0)
-        square_on_scalar((last, 0, 0))
+            apply_gain(*gains_now[1])
+            transform(k + 1, range(HALVES) if k + 1 < last else [0])
+            root(*sums_now[0])
+            root(*sums_now[1])
         turn(last - 1, 1)
+        copy_on_vector((last, 0, 0))
+        square_on_scalar((last, 1, 0))
         turn(last - 1, 0)
         apply_gain(last - 2, 1)
-        quantise(last - 3)
-        square_on_scalar((last, 1, 0))
-        apply_gain(last - 2, 0)
-        filter_bank(last - 4)
-        store(last - 4)
+        square_on_vector((last, 0, 0))
+        transform(last, [1])
         root(last - 1, 1)
-        quantise(last - 2)
-        square_on_scalar((last, 0, 1))
-        turn(last, 0)
+        filter_wide()
+        quantise(last - 3)
+        apply_gain(last - 2, 0)
         root(last - 1, 0)
-        add_transposed(last, 1, [squares[(last, 0, 1)]], last=False)
+        square_on_scalar((last, 0, 1))
         apply_gain(last - 1, 1)
+        turn(last, 0)
+        quantise(last - 2)
         square_on_scalar((last, 1, 1))
-        add_transposed(last, 1, [squares[(last, 1, 1)]], first=False)
+        apply_gain(last - 1, 0)
+        turn(last, 1)
+        store(last - 4)
         filter_bank(last - 3)
         filter_bank(last - 2)
-        apply_gain(last - 1, 0)
-        root(last, 0)
         quantise(last - 1)
+        root(last, 0)
+        filter_bank(last - 1)
         root(last, 1, 2)
         apply_gain(last, 0)
-        filter_bank(last - 1)
+        store(last - 1)
         quantise(last, 0, 1)
         apply_gain(last, 1, 2)
-        store(last - 1)
         quantise(last, 1, 1)
         filter_bank(last)
         store(last)

@@ -111,7 +111,14 @@ def tile_list_meltab_mix_mag_kernel(
 
         def gather_words(piece):
             codes = keep.tile([P, PIECE], U32, name=f"picked_codes{piece}", align_bytes=64)
-            nc.vector.tensor_copy(codes[:], table[:].bitcast(U32).indirect(piece_offsets(piece)))
+            parts = 2 if piece == 0 else 1
+            width = PIECE // parts
+            for i in range(parts):
+                first = (piece * PIECE + i * width) // 16
+                nc.vector.tensor_copy(
+                    codes[:, i * width : (i + 1) * width],
+                    table[:].bitcast(U32).indirect(offsets[:, first : first + width // 16]),
+                )
             picked_codes[piece] = codes
 
         filters = {}
@@ -133,7 +140,8 @@ def tile_list_meltab_mix_mag_kernel(
         def transform(k, halves=range(HALVES), kinds=range(2)):
             codes, plane = picked_codes[k * P // PIECE], picked_planes[k * P // PIECE]
             tokens = slice(k * P % PIECE, k * P % PIECE + P)
-            for c, b in [(c, b) for b in halves for c in kinds]:
+            order = [(c, b) for b in halves for c in kinds]
+            for c, b in order if k < 3 else reversed(order):
                 weight_plane, row = ((co_plane, CO_ROW), (si_plane, SI_ROW))[c]
                 freqs = slice(b * HALF, (b + 1) * HALF)
                 part = psum.tile([P, HALF], F32, name="part", bufs=PART_BANKS)
@@ -153,7 +161,7 @@ def tile_list_meltab_mix_mag_kernel(
             for i in range(WARM_PASSES):
                 nc.tensor.matmul_mx(
                     out=scratch[:], lhsT=co_first[:, 0:P].bitcast(FP8X4), lhsT_scale=picked_planes[0][:, 0:P],
-                    rhs=co_first[:, 0:PIECE].bitcast(FP8X4), rhs_scale=picked_planes[1][:], start=True, stop=True,
+                    rhs=co_first[:, 0:PIECE].bitcast(FP8X4), rhs_scale=picked_planes[0][:], start=True, stop=True,
                 )
 
         def new_square(key):
@@ -325,39 +333,38 @@ def tile_list_meltab_mix_mag_kernel(
         for k in range(3, last):
             sums_now = early_sums.get(k, ((k - 1, 1), (k - 1, 0)))
             gains_now = early_gains.get(k, ((k - 2, 1), (k - 2, 0)))
-            copy_on_vector((k, 0, 0))
             square_on_scalar((k, 1, 0))
+            apply_gain(*gains_now[0])
             turn(*sums_now[0])
             turn(*sums_now[1])
-            apply_gain(*gains_now[0])
-            square_on_vector((k, 0, 0))
+            copy_on_vector((k, 0, 0))
             square_on_scalar((k, 0, 1))
-            quantise_pair(*{3: (0, 0), 4: (0, 1), 5: (2, 1), 6: (2, 0)}[k])
-            square_on_scalar((k, 1, 1))
             apply_gain(*gains_now[1])
+            square_on_scalar((k, 1, 1))
+            square_on_vector((k, 0, 0))
+            quantise_pair(*{3: (0, 0), 4: (0, 1), 5: (2, 1), 6: (2, 0)}[k])
             transform(k + 1, range(HALVES) if k + 1 < last else [0])
-            root(*sums_now[0])
             root(*sums_now[1])
+            root(*sums_now[0])
         turn(last - 1, 1)
-        copy_on_vector((last, 0, 0))
+        square_on_scalar((last, 0, 0))
         square_on_scalar((last, 1, 0))
         turn(last - 1, 0)
         apply_gain(last - 2, 1)
-        square_on_vector((last, 0, 0))
         transform(last, [1])
-        root(last - 1, 1)
         filter_wide()
         quantise(last - 3)
         apply_gain(last - 2, 0)
-        root(last - 1, 0)
+        root(last - 1, 1)
+        store(last - 4)
         square_on_scalar((last, 0, 1))
-        apply_gain(last - 1, 1)
         turn(last, 0)
         quantise(last - 2)
+        apply_gain(last - 1, 1)
         square_on_scalar((last, 1, 1))
-        apply_gain(last - 1, 0)
         turn(last, 1)
-        store(last - 4)
+        root(last - 1, 0)
+        apply_gain(last - 1, 0)
         filter_bank(last - 3)
         filter_bank(last - 2)
         quantise(last - 1)

@@ -15,7 +15,6 @@ FP8X4 = mybir.dt.float8_e4m3fn_x4
 FP4X4 = mybir.dt.float4_e2m1fn_x4
 ACT = mybir.ActivationFunctionType
 MULT = mybir.AluOpType.mult
-ADD = mybir.AluOpType.add
 
 P = 128
 PACK = 4
@@ -24,11 +23,14 @@ HALVES = F // HALF
 TILES = J // P
 PIECE = 256
 CO_ROW, SI_ROW = 4, 8
-PART_BANKS = 6
+PART_BANKS = 5
+POWER_BANKS = 2
 EDGE = 16
 WIDE = 4
+SPARE_PARTS = ((2, 1, 0), (2, 1, 1))
+GPSIMD_GAINS = ((0, 0), (1, 0), (2, 0), (0, 1), (1, 1))
+DOUBLE_TILES = (4,)
 WARM_PASSES = 7
-GPSIMD_TILES = ()
 STORES = ((0, 3), (4, 6), (7, 7))
 
 
@@ -59,7 +61,6 @@ def tile_list_meltab_mix_mag_kernel(
         identity = keep.tile([P, P], F32, name="identity")
         warm_in = keep.tile([P, 1], F32, name="warm_in", tag="gain")
         warm_out = keep.tile([P, 1], F32, name="warm_out")
-        result = keep.tile([P, J], F32, name="result")
 
         def words(dram):
             return dram[0].rearrange("p n t -> p (n t)").bitcast(I32)
@@ -110,7 +111,8 @@ def tile_list_meltab_mix_mag_kernel(
             picked_planes[piece] = plane
 
         def gather_words(piece):
-            codes = keep.tile([P, PIECE], U32, name=f"picked_codes{piece}", align_bytes=64)
+            tag = "square0_1_0" if piece == J // PIECE - 1 else f"picked_codes{piece}"
+            codes = keep.tile([P, PIECE], U32, name=f"picked_codes{piece}", tag=tag, align_bytes=64)
             parts = 2 if piece == 0 else 1
             width = PIECE // parts
             for i in range(parts):
@@ -135,16 +137,19 @@ def tile_list_meltab_mix_mag_kernel(
             load_scale_rows(nc.sync, filters["fb8_plane"], 0, fb8_scales[0], range(4))
             load_scale_rows(nc.sync, filters["fb4_plane"], 0, fb4_scales[0], range(4))
 
-        parts, squares, plains, added, powers, mags, hs, quantised, sums = {}, {}, {}, {}, {}, {}, {}, {}, {}
+        parts, squares, powers, mags, hs, quantised, sums = {}, {}, {}, {}, {}, {}, {}
 
         def transform(k, halves=range(HALVES), kinds=range(2)):
             codes, plane = picked_codes[k * P // PIECE], picked_planes[k * P // PIECE]
             tokens = slice(k * P % PIECE, k * P % PIECE + P)
             order = [(c, b) for b in halves for c in kinds]
-            for c, b in order if k < 3 else reversed(order):
+            for c, b in order:
                 weight_plane, row = ((co_plane, CO_ROW), (si_plane, SI_ROW))[c]
                 freqs = slice(b * HALF, (b + 1) * HALF)
-                part = psum.tile([P, HALF], F32, name="part", bufs=PART_BANKS)
+                if (k, c, b) in SPARE_PARTS:
+                    part = psum.tile([P, HALF], F32, name="spare")
+                else:
+                    part = psum.tile([P, HALF], F32, name="part", bufs=PART_BANKS)
                 parts[(k, c, b)] = part[:].rearrange("p (m t) -> p t m", t=PACK)
                 nc.tensor.matmul_mx(
                     out=part[:],
@@ -157,7 +162,7 @@ def tile_list_meltab_mix_mag_kernel(
                 )
 
         def warm_tensor():
-            scratch = psum.tile([P, PIECE], F32, name="power", bufs=2)
+            scratch = psum.tile([P, PIECE], F32, name="power", bufs=POWER_BANKS)
             for i in range(WARM_PASSES):
                 nc.tensor.matmul_mx(
                     out=scratch[:], lhsT=co_first[:, 0:P].bitcast(FP8X4), lhsT_scale=picked_planes[0][:, 0:P],
@@ -165,32 +170,23 @@ def tile_list_meltab_mix_mag_kernel(
                 )
 
         def new_square(key):
-            squares[key] = keep.tile([P, PACK, P], F32, name="square%d_%d_%d" % key)
+            squares[key] = keep.tile([P, PACK, P], F32, name="square%d_%d_%d" % key, align_bytes=64)
             return squares[key]
 
         def square_on_scalar(key):
             nc.scalar.activation(out=new_square(key)[:], in_=parts[key], func=ACT.Square)
 
-        def copy_on_vector(key):
-            plains[key] = keep.tile([P, PACK, P], F32, name="plain%d_%d_%d" % key)
-            nc.vector.tensor_copy(out=plains[key][:], in_=parts[key])
-
         def square_on_vector(key):
-            nc.vector.tensor_tensor(out=new_square(key)[:], in0=parts[key], in1=plains[key][:], op=MULT)
-
-        def add_on_gpsimd(k):
-            tag = f"h{k - 3}" if k >= 3 else f"mag{k - 2}_0"
-            added[k] = keep.tile([P, PACK, P], F32, name=f"added{k}", tag=tag, align_bytes=64)
-            for slots in (slice(0, PACK // 2), slice(PACK // 2, PACK)):
-                nc.gpsimd.tensor_tensor(
-                    out=added[k][:, slots], in0=squares[(k, 0, 0)][:, slots], in1=squares[(k, 1, 0)][:, slots], op=ADD
-                )
+            twice = parts[key].unsqueeze(3).to_broadcast([P, PACK, P, 2])
+            nc.vector.tensor_reduce(out=new_square(key)[:], in_=twice, axis=mybir.AxisListType.X, op=MULT)
 
         def add_transposed(k, b, terms, first=True, last=True):
-            if first and k == TILES - 1:
+            if first and (k, b) == (TILES - 1, 1):
                 powers[(k, b)] = psum.tile([P, PACK, P], F32, name="part", bufs=PART_BANKS)
+            elif first and len(powers) >= 4 and len(powers) % 3 == 1:
+                powers[(k, b)] = psum.tile([P, PACK, P], F32, name="spare")
             elif first:
-                powers[(k, b)] = psum.tile([P, PACK, P], F32, name="power", bufs=2)
+                powers[(k, b)] = psum.tile([P, PACK, P], F32, name="power", bufs=POWER_BANKS)
             for t in range(PACK):
                 for c, term in enumerate(terms):
                     whole = first and last
@@ -202,10 +198,7 @@ def tile_list_meltab_mix_mag_kernel(
                     )
 
         def turn(k, b):
-            if b == 0 and k in added:
-                add_transposed(k, b, [added[k]])
-            else:
-                add_transposed(k, b, [squares[(k, c, b)] for c in (1, 0)])
+            add_transposed(k, b, [squares[(k, c, b)] for c in (1, 0)])
 
         def root(k, b, pieces=1):
             mags[(k, b)] = keep.tile([P, P, PACK], F32, name=f"mag{k}_{b}", align_bytes=64)
@@ -227,19 +220,19 @@ def tile_list_meltab_mix_mag_kernel(
                 plane = keep.tile([P, HALVES * P], U8, name=f"h_plane{k}", align_bytes=64)
                 quantised[k] = (codes, plane)
             h = wide_h[b][:, k] if k < WIDE else hs[k][:, b]
+            engine = nc.gpsimd if (k, b) in GPSIMD_GAINS else nc.vector
             for i in range(pieces):
                 tokens = slice(i * P // pieces, (i + 1) * P // pieces)
-                nc.vector.tensor_tensor(
+                engine.tensor_tensor(
                     out=h[:, tokens], in0=mags[(k, b)][:, tokens],
                     in1=gain[:, b : b + 1, :].to_broadcast([P, P // pieces, PACK]), op=MULT,
                 )
 
-        def quantise_pair(k, b):
-            cols = slice(k * P, (k + 2) * P)
+        def quantise_wide(b):
             nc.vector.quantize_mx(
-                out=wide_codes[b][:, cols].bitcast(FP8X4),
-                scales=wide_plane[b][:, cols],
-                in_=wide_h[b][:, k : k + 2].rearrange("p k j t -> p (k j t)"),
+                out=wide_codes[b][:].bitcast(FP8X4),
+                scales=wide_plane[b][:],
+                in_=wide_h[b][:].rearrange("p k j t -> p (k j t)"),
             )
 
         def quantise(k, first_half=0, halves=HALVES):
@@ -251,130 +244,124 @@ def tile_list_meltab_mix_mag_kernel(
                 in_=hs[k][:, first_half : first_half + halves].rearrange("p b j t -> p (b j t)"),
             )
 
-        def filter_passes(y, low, low_plane, high, high_plane):
+        def filter_pass(b, y, codes, plane):
+            name, dtype = (("fb8", FP8X4), ("fb4", FP4X4))[b]
             nc.tensor.matmul_mx(
-                out=y, lhsT=filters["fb8"].bitcast(FP8X4), lhsT_scale=filters["fb8_plane"],
-                rhs=low.bitcast(FP8X4), rhs_scale=low_plane, start=True, stop=False,
-            )
-            nc.tensor.matmul_mx(
-                out=y, lhsT=filters["fb4"].bitcast(FP4X4), lhsT_scale=filters["fb4_plane"],
-                rhs=high.bitcast(FP8X4), rhs_scale=high_plane, start=False, stop=True,
+                out=y, lhsT=filters[name].bitcast(dtype), lhsT_scale=filters[name + "_plane"],
+                rhs=codes.bitcast(FP8X4), rhs_scale=plane, start=(b == 0), stop=(b == HALVES - 1),
             )
 
-        def filter_wide():
-            sums[0] = psum.tile([P, WIDE * P], F32, name="part", bufs=PART_BANKS)
-            filter_passes(sums[0][:], wide_codes[0][:], wide_plane[0][:], wide_codes[1][:], wide_plane[1][:])
+        def filter_wide(b):
+            if b == 0:
+                sums[0] = psum.tile([P, WIDE * P], F32, name="part", bufs=PART_BANKS)
+            filter_pass(b, sums[0][:], wide_codes[b][:], wide_plane[b][:])
 
         def filter_bank(k):
             codes, plane = quantised[k]
             first, last = [(a, z) for a, z in STORES if a <= k <= z][0]
-            if k == TILES - 1:
-                sums[first] = psum.tile([P, P], F32, name="power", bufs=2)
-            elif k == first:
+            if k == first:
                 sums[first] = psum.tile([P, (last - first + 1) * P], F32, name="part", bufs=PART_BANKS)
             cols = slice((k - first) * P, (k - first + 1) * P)
-            filter_passes(sums[first][:, cols], codes[:, 0:P], plane[:, 0:P], codes[:, P : 2 * P], plane[:, P : 2 * P])
+            for b in range(HALVES):
+                filter_pass(b, sums[first][:, cols], codes[:, b * P : (b + 1) * P], plane[:, b * P : (b + 1) * P])
 
         def store(k):
             for first, last in STORES:
                 if k == last:
                     tokens = slice(first * P, (last + 1) * P)
-                    if first == 0:
-                        nc.vector.tensor_copy(out=result[:, tokens], in_=sums[first][:])
-                    else:
-                        nc.scalar.copy(out=result[:, tokens], in_=sums[first][:])
-                    nc.sync.dma_start(out=out[:, tokens], in_=result[:, tokens])
+                    tag = "square%d_1_1" % (TILES - 1) if first == 0 else f"result{first}"
+                    result = keep.tile([P, (last - first + 1) * P], F32, name=f"result{first}", tag=tag, align_bytes=64)
+                    nc.scalar.copy(out=result[:], in_=sums[first][:])
+                    nc.sync.dma_start(out=out[:, tokens], in_=result[:])
 
         last = TILES - 1
         for piece in range(J // PIECE):
             gather_scales(piece)
         warm_tensor()
-        for piece in range(J // PIECE):
+        for piece in range(J // PIECE - 1):
             gather_words(piece)
-        transform(0, [0])
-        transform(1, [0])
-        transform(2, [0], [0])
+        for k in range(3):
+            transform(k, [0])
         square_on_scalar((0, 0, 0))
-        transform(2, [0], [1])
         square_on_scalar((0, 1, 0))
-        copy_on_vector((1, 0, 0))
-        transform(0, [1], [0])
-        copy_on_vector((2, 0, 0))
-        square_on_scalar((1, 1, 0))
         square_on_vector((1, 0, 0))
-        turn(0, 0)
-        transform(1, [1], [0])
+        square_on_scalar((1, 1, 0))
         square_on_vector((2, 0, 0))
         square_on_scalar((2, 1, 0))
-        transform(0, [1], [1])
-        transform(1, [1], [1])
-        copy_on_vector((0, 0, 1))
-        root(0, 0)
+        transform(0, [1], [0])
+        turn(0, 0)
         turn(1, 0)
-        copy_on_vector((1, 0, 1))
-        square_on_scalar((0, 1, 1))
-        square_on_vector((0, 0, 1))
+        gather_words(J // PIECE - 1)
+        transform(0, [1], [1])
+        transform(1, [1])
         transform(2, [1])
+        root(0, 0)
         root(1, 0)
-        square_on_vector((1, 0, 1))
-        turn(2, 0)
-        square_on_scalar((1, 1, 1))
+        for k in range(3):
+            square_on_vector((k, 0, 1))
+            square_on_scalar((k, 1, 1))
         apply_gain(0, 0)
-        square_on_scalar((2, 0, 1))
-        turn(0, 1)
-        root(2, 0)
         apply_gain(1, 0)
-        square_on_scalar((2, 1, 1))
+        turn(2, 0)
+        turn(0, 1)
         transform(3)
         load_filters()
+        root(2, 0)
         root(0, 1)
-        early_sums = {3: ((1, 1), (2, 1))}
-        early_gains = {3: ((0, 1), (2, 0)), 4: ((1, 1), (2, 1))}
+        apply_gain(2, 0)
+        apply_gain(0, 1)
         for k in range(3, last):
-            sums_now = early_sums.get(k, ((k - 1, 1), (k - 1, 0)))
-            gains_now = early_gains.get(k, ((k - 2, 1), (k - 2, 0)))
+            sums_now = ((1, 1), (2, 1)) if k == 3 else ((k - 1, 1), (k - 1, 0))
+            gains_now = {3: (), 4: ((1, 1), (2, 1))}.get(k, ((k - 2, 1), (k - 2, 0)))
+            square_on_vector((k, 0, 0))
+            if k in DOUBLE_TILES:
+                square_on_vector((k, 0, 1))
+            for key in gains_now:
+                apply_gain(*key)
             square_on_scalar((k, 1, 0))
-            apply_gain(*gains_now[0])
+            square_on_scalar((k, 1, 1))
+            if k not in DOUBLE_TILES:
+                square_on_scalar((k, 0, 1))
             turn(*sums_now[0])
             turn(*sums_now[1])
-            copy_on_vector((k, 0, 0))
-            square_on_scalar((k, 0, 1))
-            apply_gain(*gains_now[1])
-            square_on_scalar((k, 1, 1))
-            square_on_vector((k, 0, 0))
-            quantise_pair(*{3: (0, 0), 4: (0, 1), 5: (2, 1), 6: (2, 0)}[k])
+            if k == 5:
+                quantise_wide(1)
+                quantise_wide(0)
+            if k == 6:
+                quantise(4)
             transform(k + 1, range(HALVES) if k + 1 < last else [0])
-            root(*sums_now[1])
             root(*sums_now[0])
-        turn(last - 1, 1)
+            root(*sums_now[1])
         square_on_scalar((last, 0, 0))
         square_on_scalar((last, 1, 0))
-        turn(last - 1, 0)
         apply_gain(last - 2, 1)
-        transform(last, [1])
-        filter_wide()
-        quantise(last - 3)
         apply_gain(last - 2, 0)
+        turn(last - 1, 1)
+        transform(last, [1], [0])
+        filter_wide(0)
         root(last - 1, 1)
-        store(last - 4)
         square_on_scalar((last, 0, 1))
-        turn(last, 0)
+        turn(last - 1, 0)
+        transform(last, [1], [1])
+        filter_wide(1)
         quantise(last - 2)
         apply_gain(last - 1, 1)
-        square_on_scalar((last, 1, 1))
-        turn(last, 1)
         root(last - 1, 0)
-        apply_gain(last - 1, 0)
+        square_on_scalar((last, 1, 1))
+        turn(last, 0)
+        add_transposed(last, 1, [squares[(last, 0, 1)]], last=False)
+        add_transposed(last, 1, [squares[(last, 1, 1)]], first=False)
         filter_bank(last - 3)
         filter_bank(last - 2)
-        quantise(last - 1)
+        apply_gain(last - 1, 0)
         root(last, 0)
-        filter_bank(last - 1)
+        quantise(last - 1)
         root(last, 1, 2)
         apply_gain(last, 0)
-        store(last - 1)
-        quantise(last, 0, 1)
+        filter_bank(last - 1)
         apply_gain(last, 1, 2)
-        quantise(last, 1, 1)
+        store(last - 4)
+        store(last - 1)
+        quantise(last)
         filter_bank(last)
         store(last)

@@ -28,8 +28,8 @@ POWER_BANKS = 2
 EDGE = 16
 WIDE = 4
 SPARE_PARTS = ((2, 1, 0), (2, 1, 1))
-GPSIMD_GAINS = ((0, 0), (1, 0), (2, 0), (0, 1), (1, 1))
-DOUBLE_TILES = (4,)
+GPSIMD_GAINS = ()
+DOUBLE_TILES = ()
 WARM_PASSES = 7
 STORES = ((0, 3), (4, 6), (7, 7))
 

from contextlib import ExitStack

import concourse.mybir as mybir

K, F, N, T, J = 512, 1024, 128, 2048, 1024
FLOPS = 2 * (2 * K * F * J + F * N * J)

F32 = mybir.dt.float32
BF16 = mybir.dt.bfloat16
I32 = mybir.dt.int32
U32 = mybir.dt.uint32
U16 = mybir.dt.uint16
U8 = mybir.dt.uint8
FP8X4 = mybir.dt.float8_e4m3fn_x4
FP4X4 = mybir.dt.float4_e2m1fn_x4
ACT = mybir.ActivationFunctionType
MULT = mybir.AluOpType.mult

P = 128
PACK = 4
HALF = P * PACK
HALVES = F // HALF
TILES = J // P
PIECE = 256
CO_ROW, SI_ROW = 4, 8
PART_BANKS = 5
POWER_BANKS = 2
EDGE = 16
WIDE = 4
SPARE_PARTS = ((2, 1, 0), (2, 1, 1))
GPSIMD_GAINS = ()
DOUBLE_TILES = ()
WARM_PASSES = 7
STORES = ((0, 3), (4, 6), (7, 7))


def load_scale_rows(queue, plane, first_row, rows, quadrants):
    for q in quadrants:
        queue.dma_start(
            out=plane[32 * q + first_row : 32 * q + first_row + 4, :].bitcast(I32),
            in_=rows[4 * q : 4 * q + 4, :].bitcast(I32),
        )


def tile_list_meltab_mix_mag_kernel(
    tc, tab_words, tab_scales, co_words, co_scales, si_words, si_scales, gn,
    fb8_words, fb8_scales, fb4_words, fb4_scales, offs, out,
):
    nc = tc.nc
    with ExitStack() as ctx:
        keep = ctx.enter_context(tc.tile_pool(name="keep", bufs=1))
        psum = ctx.enter_context(tc.psum_pool(name="psum", bufs=1))

        offsets = keep.tile([P, J // 16], U16, name="offsets")
        left_zeros = keep.tile([P, EDGE], I32, name="left_zeros", tag="table", align_bytes=64)
        right_zeros = keep.tile([P, EDGE], I32, name="right_zeros", tag="later", align_bytes=64)
        table_plane = keep.tile([P, T], U8, name="table_plane", align_bytes=64)
        co_plane = keep.tile([P, F], U8, name="co_plane", align_bytes=64)
        si_plane = keep.tile([P, F], U8, name="si_plane", align_bytes=64)
        co_first = keep.tile([P, HALF], I32, name="co_first", align_bytes=64)
        identity = keep.tile([P, P], F32, name="identity")
        warm_in = keep.tile([P, 1], F32, name="warm_in", tag="gain")
        warm_out = keep.tile([P, 1], F32, name="warm_out")

        def words(dram):
            return dram[0].rearrange("p n t -> p (n t)").bitcast(I32)

        nc.vector.memset(co_plane[0:96, :].bitcast(I32), 0)
        nc.vector.memset(left_zeros[:], 0)
        nc.vector.memset(right_zeros[:], 0)
        nc.vector.memset(table_plane[:].bitcast(I32), 0)
        si_plane32 = si_plane[:].bitcast(I32)
        nc.vector.tensor_copy(out=si_plane32[:, 0:EDGE], in_=left_zeros[:])
        nc.vector.tensor_copy(out=si_plane32[:, EDGE : 2 * EDGE], in_=right_zeros[:])
        nc.vector.memset(si_plane32[:, 2 * EDGE : F // 4], 0)
        nc.vector.memset(co_plane[96:P, :].bitcast(I32), 0)
        nc.vector.memset(warm_in[:], 1.0)
        nc.vector.memset(identity[:], 0.0)
        nc.sync.dma_start(offsets[:], offs)
        nc.sync.dma_start(out=co_first[:], in_=words(co_words)[:, 0:HALF])
        load_scale_rows(nc.gpsimd, co_plane, CO_ROW, co_scales[0], range(0, 2))
        load_scale_rows(nc.scalar, co_plane, CO_ROW, co_scales[0], range(2, 3))
        load_scale_rows(nc.scalar, table_plane, 0, tab_scales[0], range(0, 2))
        load_scale_rows(nc.sync, table_plane, 0, tab_scales[0], range(2, 4))
        table = keep.tile([P, T], I32, name="table", align_bytes=64)
        nc.sync.dma_start(out=table[:], in_=words(tab_words))
        nc.scalar.activation(out=warm_out[:], in_=warm_in[:], func=ACT.Sqrt)
        load_scale_rows(nc.scalar, co_plane, CO_ROW, co_scales[0], range(3, 4))
        load_scale_rows(nc.sync, si_plane, SI_ROW, si_scales[0], range(4))
        nc.gpsimd.affine_select(
            out=identity[:], in_=identity[:], pattern=[[-1, P]], compare_op=mybir.AluOpType.not_equal, fill=1.0,
            base=0, channel_multiplier=1,
        )

        later = keep.tile([P, 3 * HALF], I32, name="later", align_bytes=64)
        gain = keep.tile([P, HALVES, PACK], F32, name="gain")
        weights = {(0, 0): co_first[:], (1, 0): later[:, 0:HALF], (0, 1): later[:, HALF:F], (1, 1): later[:, F : 3 * HALF]}
        nc.sync.dma_start(out=weights[(1, 0)], in_=words(si_words)[:, 0:HALF])
        nc.sync.dma_start(out=weights[(0, 1)], in_=words(co_words)[:, HALF:F])
        nc.sync.dma_start(out=weights[(1, 1)], in_=words(si_words)[:, HALF:F])
        nc.sync.dma_start(out=gain[:], in_=gn.rearrange("(b m t) -> m b t", b=HALVES, t=PACK))

        picked_codes, picked_planes = {}, {}

        def piece_offsets(piece):
            return offsets[:, piece * PIECE // 16 : (piece + 1) * PIECE // 16]

        def gather_scales(piece):
            plane = keep.tile([P, PIECE], U8, name=f"picked_plane{piece}", align_bytes=64)
            nc.vector.tensor_copy(plane[:], table_plane[:].indirect(piece_offsets(piece)))
            picked_planes[piece] = plane

        def gather_words(piece):
            tag = "square0_1_0" if piece == J // PIECE - 1 else f"picked_codes{piece}"
            codes = keep.tile([P, PIECE], U32, name=f"picked_codes{piece}", tag=tag, align_bytes=64)
            parts = 2 if piece == 0 else 1
            width = PIECE // parts
            for i in range(parts):
                first = (piece * PIECE + i * width) // 16
                nc.vector.tensor_copy(
                    codes[:, i * width : (i + 1) * width],
                    table[:].bitcast(U32).indirect(offsets[:, first : first + width // 16]),
                )
            picked_codes[piece] = codes

        filters = {}

        def load_filters():
            tile = keep.tile([P, 2 * N], I32, name="filters", tag="picked_plane0", align_bytes=64)
            filters["fb8"] = tile[:, 0:N]
            filters["fb4"] = tile[:, N : N + N // 2].bitcast(U8)
            filters["fb8_plane"] = tile[:, N + N // 2 : N + N // 2 + N // 4].bitcast(U8)
            filters["fb4_plane"] = tile[:, N + N // 2 + N // 4 : 2 * N].bitcast(U8)
            nc.gpsimd.memset(tile[:], 0)
            nc.sync.dma_start(out=filters["fb8"], in_=words(fb8_words))
            nc.sync.dma_start(out=filters["fb4"].bitcast(I32), in_=fb4_words[0].bitcast(I32))
            load_scale_rows(nc.sync, filters["fb8_plane"], 0, fb8_scales[0], range(4))
            load_scale_rows(nc.sync, filters["fb4_plane"], 0, fb4_scales[0], range(4))

        parts, squares, powers, mags, hs, quantised, sums = {}, {}, {}, {}, {}, {}, {}

        def transform(k, halves=range(HALVES), kinds=range(2)):
            codes, plane = picked_codes[k * P // PIECE], picked_planes[k * P // PIECE]
            tokens = slice(k * P % PIECE, k * P % PIECE + P)
            order = [(c, b) for b in halves for c in kinds]
            for c, b in order:
                weight_plane, row = ((co_plane, CO_ROW), (si_plane, SI_ROW))[c]
                freqs = slice(b * HALF, (b + 1) * HALF)
                if (k, c, b) in SPARE_PARTS:
                    part = psum.tile([P, HALF], F32, name="spare")
                else:
                    part = psum.tile([P, HALF], F32, name="part", bufs=PART_BANKS)
                parts[(k, c, b)] = part[:].rearrange("p (m t) -> p t m", t=PACK)
                nc.tensor.matmul_mx(
                    out=part[:],
                    lhsT=codes[:, tokens].bitcast(FP8X4),
                    lhsT_scale=plane[:, tokens],
                    rhs=weights[(c, b)].bitcast(FP8X4),
                    rhs_scale=weight_plane[row:P, freqs],
                    start=True,
                    stop=True,
                )

        def warm_tensor():
            scratch = psum.tile([P, PIECE], F32, name="power", bufs=POWER_BANKS)
            for i in range(WARM_PASSES):
                nc.tensor.matmul_mx(
                    out=scratch[:], lhsT=co_first[:, 0:P].bitcast(FP8X4), lhsT_scale=picked_planes[0][:, 0:P],
                    rhs=co_first[:, 0:PIECE].bitcast(FP8X4), rhs_scale=picked_planes[0][:], start=True, stop=True,
                )

        def new_square(key):
            squares[key] = keep.tile([P, PACK, P], F32, name="square%d_%d_%d" % key, align_bytes=64)
            return squares[key]

        def square_on_scalar(key):
            nc.scalar.activation(out=new_square(key)[:], in_=parts[key], func=ACT.Square)

        def square_on_vector(key):
            twice = parts[key].unsqueeze(3).to_broadcast([P, PACK, P, 2])
            nc.vector.tensor_reduce(out=new_square(key)[:], in_=twice, axis=mybir.AxisListType.X, op=MULT)

        def add_transposed(k, b, terms, first=True, last=True):
            if first and (k, b) == (TILES - 1, 1):
                powers[(k, b)] = psum.tile([P, PACK, P], F32, name="part", bufs=PART_BANKS)
            elif first and len(powers) >= 4 and len(powers) % 3 == 1:
                powers[(k, b)] = psum.tile([P, PACK, P], F32, name="spare")
            elif first:
                powers[(k, b)] = psum.tile([P, PACK, P], F32, name="power", bufs=POWER_BANKS)
            for t in range(PACK):
                for c, term in enumerate(terms):
                    whole = first and last
                    nc.tensor.matmul(
                        out=powers[(k, b)][:, t, :], lhsT=term[:, t, :], rhs=identity[:],
                        start=(c == 0 if whole else first and t == 0),
                        stop=(c == len(terms) - 1 if whole else last and t == PACK - 1),
                        is_transpose=True,
                    )

        def turn(k, b):
            add_transposed(k, b, [squares[(k, c, b)] for c in (1, 0)])

        def root(k, b, pieces=1):
            mags[(k, b)] = keep.tile([P, P, PACK], F32, name=f"mag{k}_{b}", align_bytes=64)
            for i in range(pieces):
                tokens = slice(i * P // pieces, (i + 1) * P // pieces)
                nc.scalar.activation(
                    out=mags[(k, b)][:, tokens], in_=powers[(k, b)][:].rearrange("p t j -> p j t")[:, tokens],
                    func=ACT.Sqrt,
                )

        wide_h = [keep.tile([P, WIDE, P, PACK], BF16, name=f"wide_h{b}", align_bytes=64) for b in range(HALVES)]
        wide_codes = [keep.tile([P, WIDE * P], U32, name=f"wide_codes{b}", align_bytes=64) for b in range(HALVES)]
        wide_plane = [keep.tile([P, WIDE * P], U8, name=f"wide_plane{b}", align_bytes=64) for b in range(HALVES)]

        def apply_gain(k, b, pieces=1):
            if k >= WIDE and k not in hs:
                hs[k] = keep.tile([P, HALVES, P, PACK], BF16, name=f"h{k}", align_bytes=64)
                codes = keep.tile([P, HALVES * P], U32, name=f"h_codes{k}", align_bytes=64)
                plane = keep.tile([P, HALVES * P], U8, name=f"h_plane{k}", align_bytes=64)
                quantised[k] = (codes, plane)
            h = wide_h[b][:, k] if k < WIDE else hs[k][:, b]
            engine = nc.gpsimd if (k, b) in GPSIMD_GAINS else nc.vector
            for i in range(pieces):
                tokens = slice(i * P // pieces, (i + 1) * P // pieces)
                engine.tensor_tensor(
                    out=h[:, tokens], in0=mags[(k, b)][:, tokens],
                    in1=gain[:, b : b + 1, :].to_broadcast([P, P // pieces, PACK]), op=MULT,
                )

        def quantise_wide(b):
            nc.vector.quantize_mx(
                out=wide_codes[b][:].bitcast(FP8X4),
                scales=wide_plane[b][:],
                in_=wide_h[b][:].rearrange("p k j t -> p (k j t)"),
            )

        def quantise(k, first_half=0, halves=HALVES):
            codes, plane = quantised[k]
            cols = slice(first_half * P, (first_half + halves) * P)
            nc.vector.quantize_mx(
                out=codes[:, cols].bitcast(FP8X4),
                scales=plane[:, cols],
                in_=hs[k][:, first_half : first_half + halves].rearrange("p b j t -> p (b j t)"),
            )

        def filter_pass(b, y, codes, plane):
            name, dtype = (("fb8", FP8X4), ("fb4", FP4X4))[b]
            nc.tensor.matmul_mx(
                out=y, lhsT=filters[name].bitcast(dtype), lhsT_scale=filters[name + "_plane"],
                rhs=codes.bitcast(FP8X4), rhs_scale=plane, start=(b == 0), stop=(b == HALVES - 1),
            )

        def filter_wide(b):
            if b == 0:
                sums[0] = psum.tile([P, WIDE * P], F32, name="part", bufs=PART_BANKS)
            filter_pass(b, sums[0][:], wide_codes[b][:], wide_plane[b][:])

        def filter_bank(k):
            codes, plane = quantised[k]
            first, last = [(a, z) for a, z in STORES if a <= k <= z][0]
            if k == first:
                sums[first] = psum.tile([P, (last - first + 1) * P], F32, name="part", bufs=PART_BANKS)
            cols = slice((k - first) * P, (k - first + 1) * P)
            for b in range(HALVES):
                filter_pass(b, sums[first][:, cols], codes[:, b * P : (b + 1) * P], plane[:, b * P : (b + 1) * P])

        def store(k):
            for first, last in STORES:
                if k == last:
                    tokens = slice(first * P, (last + 1) * P)
                    tag = "square%d_1_1" % (TILES - 1) if first == 0 else f"result{first}"
                    result = keep.tile([P, (last - first + 1) * P], F32, name=f"result{first}", tag=tag, align_bytes=64)
                    nc.scalar.copy(out=result[:], in_=sums[first][:])
                    nc.sync.dma_start(out=out[:, tokens], in_=result[:])

        last = TILES - 1
        for piece in range(J // PIECE):
            gather_scales(piece)
        warm_tensor()
        for piece in range(J // PIECE - 1):
            gather_words(piece)
        for k in range(3):
            transform(k, [0])
        square_on_scalar((0, 0, 0))
        square_on_scalar((0, 1, 0))
        square_on_vector((1, 0, 0))
        square_on_scalar((1, 1, 0))
        square_on_vector((2, 0, 0))
        square_on_scalar((2, 1, 0))
        transform(0, [1], [0])
        turn(0, 0)
        turn(1, 0)
        gather_words(J // PIECE - 1)
        transform(0, [1], [1])
        transform(1, [1])
        transform(2, [1])
        root(0, 0)
        root(1, 0)
        for k in range(3):
            square_on_vector((k, 0, 1))
            square_on_scalar((k, 1, 1))
        apply_gain(0, 0)
        apply_gain(1, 0)
        turn(2, 0)
        turn(0, 1)
        transform(3)
        load_filters()
        root(2, 0)
        root(0, 1)
        apply_gain(2, 0)
        apply_gain(0, 1)
        for k in range(3, last):
            sums_now = ((1, 1), (2, 1)) if k == 3 else ((k - 1, 1), (k - 1, 0))
            gains_now = {3: (), 4: ((1, 1), (2, 1))}.get(k, ((k - 2, 1), (k - 2, 0)))
            square_on_vector((k, 0, 0))
            if k in DOUBLE_TILES:
                square_on_vector((k, 0, 1))
            for key in gains_now:
                apply_gain(*key)
            square_on_scalar((k, 1, 0))
            square_on_scalar((k, 1, 1))
            if k not in DOUBLE_TILES:
                square_on_scalar((k, 0, 1))
            turn(*sums_now[0])
            turn(*sums_now[1])
            if k == 5:
                quantise_wide(1)
                quantise_wide(0)
            if k == 6:
                quantise(4)
            transform(k + 1, range(HALVES) if k + 1 < last else [0])
            root(*sums_now[0])
            root(*sums_now[1])
        square_on_scalar((last, 0, 0))
        square_on_scalar((last, 1, 0))
        apply_gain(last - 2, 1)
        apply_gain(last - 2, 0)
        turn(last - 1, 1)
        transform(last, [1], [0])
        filter_wide(0)
        root(last - 1, 1)
        square_on_scalar((last, 0, 1))
        turn(last - 1, 0)
        transform(last, [1], [1])
        filter_wide(1)
        quantise(last - 2)
        apply_gain(last - 1, 1)
        root(last - 1, 0)
        square_on_scalar((last, 1, 1))
        turn(last, 0)
        add_transposed(last, 1, [squares[(last, 0, 1)]], last=False)
        add_transposed(last, 1, [squares[(last, 1, 1)]], first=False)
        filter_bank(last - 3)
        filter_bank(last - 2)
        apply_gain(last - 1, 0)
        root(last, 0)
        quantise(last - 1)
        root(last, 1, 2)
        apply_gain(last, 0)
        filter_bank(last - 1)
        apply_gain(last, 1, 2)
        store(last - 4)
        store(last - 1)
        quantise(last)
        filter_bank(last)
        store(last)
